import numpy as np
import ml_dtypes


def mxq(x, axis, fmt="e4m3"):
    dtype, down = {"e4m3": (ml_dtypes.float8_e4m3fn, 7), "e5m2": (ml_dtypes.float8_e5m2, 14)}[fmt]
    v = np.moveaxis(np.asarray(x, np.float32).astype(ml_dtypes.bfloat16).astype(np.float64), axis, -1)
    blocks = v.reshape(v.shape[:-1] + (-1, 32))
    amax = np.abs(blocks).max(-1, keepdims=True)
    byte = np.maximum(np.where(amax > 0, np.frexp(amax)[1] - 1 + 127, 0) - down, 1)
    scale = np.exp2(byte - 127.0)
    codes = (blocks / scale).astype(np.float32).astype(dtype).astype(np.float64)
    return np.moveaxis((codes * scale).reshape(v.shape), -1, axis)


WIDE = False


def mx_kscale(k):
    if not WIDE:
        return np.ones(k)
    levels = np.array([10, -10, 5, -5, 0])
    if k % 512:
        return np.exp2(np.random.permutation(np.resize(levels, k // 32))).repeat(32)
    a = np.empty((k // 512, 16))
    for p in range(k // 512):
        a[p, :8] = np.random.permutation(np.resize(levels, 8))
        for g in range(8):
            far = levels[np.abs(levels - a[p, g]) >= 10]
            a[p, g + 8] = far[np.random.randint(len(far))]
    return np.exp2(a.ravel()).repeat(32)


def f64(x):
    return np.asarray(x).astype(np.float64)


def striped(idx):
    return np.tile(idx.reshape(-1, 16).T, (8, 1)).astype(np.uint16)


def unstriped(offs):
    return offs[:16].T.reshape(-1).astype(np.int64)


E2M1 = np.array([0.0, 0.5, 1.0, 1.5, 2.0, 3.0, 4.0, 6.0, -0.0, -0.5, -1.0, -1.5, -2.0, -3.0, -4.0, -6.0])


def pack_weight(w, fmt):
    k, n = w.shape
    w = f64(np.asarray(w, np.float32).astype(ml_dtypes.bfloat16)).reshape(k // 32, 32, n)
    amax = np.abs(w).max(1)
    if fmt == "e4m3":
        byte = np.frexp(amax)[1] - 1 + 127 - 7
    else:
        mant, ex = np.frexp(amax / 6.0)
        byte = np.where(mant > 0.5, ex, ex - 1) + 127
    byte = np.clip(np.where(amax > 0, byte, 1), 1, 254)
    scaled = (w * np.exp2(127.0 - byte)[:, None, :]).reshape(k, n).astype(np.float32)
    by_word = np.ascontiguousarray(scaled.reshape(k // 512, 128, 4, n).transpose(0, 1, 3, 2))
    if fmt == "e4m3":
        words = by_word.astype(ml_dtypes.float8_e4m3fn).view(np.uint8)
    else:
        c = by_word.astype(ml_dtypes.float4_e2m1fn).view(np.uint8) & 0xF
        words = (c[..., 0::2] | (c[..., 1::2] << 4)).reshape(k // 512, 128, 2 * n)
    return np.ascontiguousarray(words), np.ascontiguousarray(byte.astype(np.uint8).reshape(k // 512, 16, n))


def unpack_weight(words, scales, fmt):
    g, _, n = scales.shape
    words = np.ascontiguousarray(words).reshape(g, 128, n, -1)
    if fmt == "e4m3":
        vals = words.view(ml_dtypes.float8_e4m3fn).astype(np.float64)
    else:
        nib = np.empty((g, 128, n, 4), np.uint8)
        nib[..., 0::2] = words & 0xF
        nib[..., 1::2] = words >> 4
        vals = E2M1[nib]
    vals = vals * np.repeat(np.exp2(scales.astype(np.float64) - 127.0), 8, axis=1)[..., None]
    return vals.transpose(0, 1, 3, 2).reshape(g * 512, n)


def gelu(v):
    return 0.5 * v * (1.0 + np.tanh(np.sqrt(2.0 / np.pi) * (v + 0.044715 * v**3)))


K, T, E, C, H, N = 1536, 512, 4, 128, 512, 384


def by_expert(wq, xq):
    return np.concatenate([wq[e].T @ xq[:, e * C:(e + 1) * C] for e in range(E)], axis=1)


def setup_inputs():
    n = np.random.standard_normal
    s = mx_kscale(K)[:, None]
    u = mx_kscale(H)
    w1 = [pack_weight(m, "e2m1") for m in n((E + 1, K, H)) / np.sqrt(K) / s[None] * u[None, None, :]]
    w2 = [pack_weight(m, "e2m1") for m in n((E + 1, H, N)) / np.sqrt(H) / u[None, :, None]]
    return {
        "xT": (n((K, T)) * s).astype(np.float32),
        "w1_words": np.stack([m[0] for m in w1]),
        "w1_scales": np.stack([m[1] for m in w1]),
        "w2_words": np.stack([m[0] for m in w2]),
        "w2_scales": np.stack([m[1] for m in w2]),
        "gate": np.tile(np.random.uniform(0.2, 1.0, E * C), (N, 1)).astype(np.float32),
        "offs": striped(np.random.permutation(T)[:E * C]),
    }


def reference(xT, w1_words, w1_scales, w2_words, w2_scales, gate, offs):
    idx = unstriped(offs)
    w1 = np.stack([unpack_weight(w1_words[e], w1_scales[e], "e2m1") for e in range(E + 1)])
    w2 = np.stack([unpack_weight(w2_words[e], w2_scales[e], "e2m1") for e in range(E + 1)])
    w1q, w2q = w1, w2
    xs = mxq(f64(xT), 0, "e4m3")
    hs = gelu(w1q[E].T @ xs)
    ys = w2q[E].T @ mxq(hs, 0, "e4m3")
    xq = mxq(f64(xT)[:, idx], 0, "e4m3")
    h = gelu(by_expert(w1q, xq))
    y = by_expert(w2q, mxq(h, 0, "e4m3"))
    out = ys
    out[:, idx] += f64(gate) * y
    return out

@@ -1,0 +1,306 @@
+from contextlib import ExitStack
+
+import concourse.mybir as mybir
+from concourse.masks import make_identity
+
+FLOPS = 2013265920
+
+K, T, E, C, H, N = 1536, 512, 4, 128, 512, 384
+P = 128
+SHARED = E
+PASSES = K // 512
+NB = N // P
+ON_GPSIMD = (1, 2, 3,)
+
+F32 = mybir.dt.float32
+BF16 = mybir.dt.bfloat16
+I32 = mybir.dt.int32
+U32 = mybir.dt.uint32
+U16 = mybir.dt.uint16
+U8 = mybir.dt.uint8
+FP8X4 = mybir.dt.float8_e4m3fn_x4
+FP4X4 = mybir.dt.float4_e2m1fn_x4
+ADD = mybir.AluOpType.add
+MULT = mybir.AluOpType.mult
+GELU = mybir.ActivationFunctionType.Gelu_apprx_tanh
+
+
+def tile_moe_shr_mlp_gelu_kernel(
+    tc, xT, w1_words, w1_scales, w2_words, w2_scales, gate, offs, out
+):
+    nc = tc.nc
+    with ExitStack() as ctx:
+        keep = ctx.enter_context(tc.tile_pool(name="keep", bufs=1))
+        work = ctx.enter_context(tc.tile_pool(name="work", bufs=2))
+        ps_l1 = ctx.enter_context(tc.psum_pool(name="ps_l1", bufs=4))
+        ps_t = ctx.enter_context(tc.psum_pool(name="ps_t", bufs=2))
+        ps_y = ctx.enter_context(tc.psum_pool(name="ps_y", bufs=1))
+
+        offsets = keep.tile([P, E * C // 16], U16, name="offsets")
+        w1_planes = keep.tile([P, (E + 1) * PASSES, H], U8, name="w1_planes", align_bytes=64)
+        w2_planes = keep.tile([P, E + 1, N], U8, name="w2_planes", align_bytes=64)
+        w2_t = keep.tile([P, E + 1, 2 * N], U8, name="w2_t", align_bytes=64)
+        w1_t = keep.tile([P, E + 1, PASSES, 2 * H], U8, name="w1_t", align_bytes=64)
+        gate_t = keep.tile([P, NB, E * C], F32, name="gate_t")
+        ident = keep.tile([P, P], F32, name="ident")
+        warm = keep.tile([P, 1], F32, name="warm")
+        warm_out = keep.tile([P, 1], F32, name="warm_out")
+        raw_0 = keep.tile([P, 3, 2, T], F32, name="raw_0")
+        raw_1 = keep.tile([P, 3, 2, T], F32, name="raw_1")
+        raw = [raw_0[:, n] for n in range(3)] + [raw_1[:, n] for n in range(3)]
+        pairs = keep.tile([P, 2 * PASSES * T * 2], BF16, name="pairs", align_bytes=64)
+        planes = [keep.tile([P, 2, E * C, 2], BF16, name=f"planes{s}", align_bytes=64) for s in range(PASSES)]
+        slots = [keep.tile([P, E * C, 4], BF16, name=f"slots{s}", align_bytes=64) for s in range(PASSES)]
+        x_codes = [keep.tile([P, E * C], U32, name=f"x_codes{s}", align_bytes=64) for s in range(PASSES)]
+        x_scales = [keep.tile([P, E * C], U8, name=f"x_scales{s}", align_bytes=64) for s in range(PASSES)]
+        out_t = [keep.tile([P, T], F32, name=f"out_t{b}") for b in range(NB)]
+
+        nc.vector.memset(w1_planes[:, 0:10, :].rearrange("p a i -> p (a i)").bitcast(I32), 0)
+        nc.gpsimd.memset(w1_planes[:, 10:15, :].rearrange("p a i -> p (a i)").bitcast(I32), 0)
+        nc.vector.memset(raw_1[:, :, 0, 0:1], 0.0)
+        nc.vector.memset(w1_t[:].bitcast(I32)[:, :, 0, 0:1], 0)
+        nc.vector.memset(w2_t[:].bitcast(I32)[:, :, 0:1], 0)
+        nc.vector.memset(gate_t[:, :, 0:1], 0.0)
+        nc.gpsimd.memset(w2_planes[:].rearrange("p a i -> p (a i)").bitcast(I32), 0)
+        make_identity(nc, ident[:])
+        nc.vector.memset(warm[:], 0.0)
+        nc.scalar.activation(warm_out[:], warm[:], GELU)
+
+        x_rows = xT.rearrange("(s p u j) t -> s u p (j t)", s=PASSES, p=P, u=2)
+        w1_src = w1_words.bitcast(I32).rearrange("e s p b -> e p s b")
+
+        def load_x(n):
+            nc.sync.dma_start(raw[n].rearrange("p j t -> p (j t)"), x_rows[n // 2, n % 2])
+
+        def load_w1(e):
+            nc.sync.dma_start(w1_t[:, e].bitcast(I32), w1_src[e])
+
+        w1_sc = w1_scales.bitcast(I32).rearrange("e s (a r) i -> r a (e s) i", r=4)
+        w2_sc = w2_scales.bitcast(I32).rearrange("e s (a r) i -> r a (e s) i", r=4)
+
+        load_x(0)
+        nc.sync.dma_start(offsets[:], offs)
+        load_x(1)
+        load_x(2)
+        for r in range(4):
+            nc.sync.dma_start(w1_planes[r:P:32].bitcast(I32), w1_sc[r])
+        load_x(3)
+        load_x(4)
+        load_w1(SHARED)
+        load_x(5)
+        load_w1(0)
+        load_w1(1)
+        nc.sync.dma_start(w2_t[:].bitcast(I32), w2_words.bitcast(I32).rearrange("e a p b -> p (e a) b"))
+        nc.sync.dma_start(gate_t[:], gate.rearrange("(b p) j -> p b j", p=P))
+        load_w1(2)
+        load_w1(3)
+
+        for r in range(4):
+            nc.gpsimd.dma_start(w2_planes[r:P:32].bitcast(I32), w2_sc[r])
+
+        def block(n):
+            return (2 * PASSES - 1 - n) * T
+
+        def cast(n, copy):
+            dst = pairs[:, 2 * block(n) : 2 * (block(n) + T)].rearrange("p (t j) -> p t j", j=2)
+            copy(dst, raw[n].rearrange("p j t -> p t j"))
+
+        def gather(n, lo, hi):
+            width = T if n == 0 else 2 * T
+            window = pairs[:, 2 * block(n) : 2 * (block(n) + width)].bitcast(U32)
+            dst = planes[n // 2][:, n % 2, lo:hi, :].rearrange("p a e -> p (a e)").bitcast(U32)
+            nc.vector.tensor_copy(dst, window.indirect(offsets[:, lo // 16 : hi // 16]))
+
+        def interleave(s, lo, hi, copy):
+            src = planes[s][:, :, lo:hi, :].bitcast(F32)[:, :, :, 0].rearrange("p u a -> p a u")
+            copy(slots[s][:, lo:hi, :].bitcast(F32), src)
+
+        def quantize_x(s, lo, hi):
+            nc.vector.quantize_mx(
+                out=x_codes[s][:, lo:hi].bitcast(FP8X4),
+                scales=x_scales[s][:, lo:hi],
+                in_=slots[s][:, lo:hi, :].rearrange("p a d -> p (a d)"),
+            )
+
+        acc = {}
+
+        def layer1(c, i, s):
+            if s == 0:
+                tile = ps_l1.tile([P, H], F32, name="acc")
+                acc[c, i] = tile
+            e = (c, SHARED)[i]
+            cols = slice(c * C, (c + 1) * C)
+            nc.tensor.matmul_mx(
+                out=acc[c, i][:],
+                lhsT=x_codes[s][:, cols].bitcast(FP8X4),
+                lhsT_scale=x_scales[s][:, cols],
+                rhs=w1_t[:, e, s, :].bitcast(FP4X4),
+                rhs_scale=w1_planes[:, e * PASSES + s, :],
+                start=(s == 0),
+                stop=(s == PASSES - 1),
+            )
+
+        h_act = {}
+
+        def activate(c, i):
+            h = work.tile([P, H], BF16, name=f"h{i}", align_bytes=64)
+            h_act[c, i] = h
+            nc.scalar.activation(h[:], acc[c, i][:], GELU)
+
+        h_rows, h_q, turned = {}, {}, {}
+
+        def turn(c, halves):
+            bank = ps_t.tile([P, 4, C], F32, name="bank")
+            for i in halves:
+                turned[c, i] = bank
+                words = h_act[c, i][:].bitcast(F32)
+                for u in range(2):
+                    nc.tensor.transpose(bank[:, 2 * i + u, :], words[:, u : H // 2 : 2], ident[:])
+
+        def group_h(c, halves, copy):
+            if c not in h_rows:
+                rows = work.tile([P, 2, C, 4], BF16, name="rows", align_bytes=64)
+                h_rows[c] = rows
+            lo, hi = halves[0], halves[-1] + 1
+            src = turned[c, lo][:, 2 * lo : 2 * hi, :].rearrange("p (i u) r -> p i r u", u=2)
+            copy(h_rows[c][:, lo:hi].bitcast(F32), src)
+
+        def quantize_h(c, halves):
+            if c not in h_q:
+                h_codes = work.tile([P, 2 * C], U32, name="h_codes", align_bytes=64)
+                h_scales = work.tile([P, 2 * C], U8, name="h_scales", align_bytes=64)
+                h_q[c] = (h_codes, h_scales)
+            lo, hi = halves[0], halves[-1] + 1
+            nc.vector.quantize_mx(
+                out=h_q[c][0][:, lo * C : hi * C].bitcast(FP8X4),
+                scales=h_q[c][1][:, lo * C : hi * C],
+                in_=h_rows[c][:, lo:hi].rearrange("p i r d -> p (i r d)"),
+            )
+
+        y = {}
+
+        def layer2(c, i):
+            y_i = ps_y.tile([P, NB, C], F32, name=f"y{i}")
+            y[c, i] = y_i
+            e = (c, SHARED)[i]
+            for b in range(NB):
+                nc.tensor.matmul_mx(
+                    out=y_i[:, b, :],
+                    lhsT=w2_t[:, e, 2 * P * b : 2 * P * (b + 1)].bitcast(FP4X4),
+                    lhsT_scale=w2_planes[:, e, P * b : P * (b + 1)],
+                    rhs=h_q[c][0][:, i * C : (i + 1) * C].bitcast(FP8X4),
+                    rhs_scale=h_q[c][1][:, i * C : (i + 1) * C],
+                    start=True,
+                    stop=True,
+                )
+
+        gated, summed = {}, {}
+
+        def gate_y(c):
+            gated_c = work.tile([P, NB, C], F32, name="gated_c")
+            gated[c] = gated_c
+            gate_c = gate_t[:, :, c * C : (c + 1) * C]
+            if c in ON_GPSIMD:
+                y_rows = work.tile([P, NB, C], F32, name="y_rows")
+                nc.scalar.copy(y_rows[:], y[c, 0][:])
+                nc.gpsimd.tensor_tensor(gated_c[:], y_rows[:], gate_c, MULT)
+            else:
+                nc.vector.tensor_tensor(gated_c[:], y[c, 0][:], gate_c, MULT)
+
+        def add_shared(c):
+            total = work.tile([P, NB, C], F32, name="total")
+            summed[c] = total
+            nc.vector.tensor_tensor(total[:], y[c, 1][:], gated[c][:], ADD)
+
+        def scatter(c, blocks):
+            for b in blocks:
+                where = offsets[:, c * C // 16 : (c + 1) * C // 16]
+                nc.vector.tensor_copy(out_t[b][:].indirect(where), summed[c][:, b, :])
+                if c == E - 1:
+                    nc.sync.dma_start(out[b * P : (b + 1) * P, :], out_t[b][:])
+
+        vec, act = nc.vector.tensor_copy, nc.scalar.copy
+        both = (0, 1)
+
+        cast(0, vec)
+        gather(0, 0, 256)
+        gather(0, 256, 512)
+        cast(1, act)
+        gather(1, 0, 512)
+        cast(2, act)
+        cast(3, act)
+        interleave(0, 0, 512, act)
+        gather(2, 0, 512)
+        gather(3, 0, 512)
+        quantize_x(0, 0, 512)
+        for i in both:
+            layer1(0, i, 0)
+        cast(4, act)
+        gather(4, 0, 128)
+        interleave(1, 0, 512, vec)
+        cast(5, act)
+        quantize_x(1, 0, 512)
+        for i in both:
+            layer1(0, i, 1)
+        gather(5, 0, 128)
+        gather(4, 128, 256)
+        interleave(2, 0, 128, vec)
+        gather(5, 128, 256)
+        quantize_x(2, 0, 128)
+        for i in both:
+            layer1(1, i, 0)
+        for i in both:
+            layer1(0, i, 2)
+            activate(0, i)
+        interleave(2, 128, 256, vec)
+        gather(4, 256, 512)
+        quantize_x(2, 128, 256)
+        for i in both:
+            layer1(1, i, 1)
+        turn(0, (0,))
+        for i in both:
+            layer1(1, i, 2)
+        turn(0, (1,))
+        group_h(0, (0,), vec)
+        group_h(0, (1,), act)
+        gather(5, 256, 512)
+        quantize_h(0, (0,))
+        interleave(2, 256, 512, vec)
+        layer2(0, 0)
+        for i in both:
+            activate(1, i)
+        quantize_h(0, (1,))
+        layer2(0, 1)
+        quantize_x(2, 256, 512)
+        gate_y(0)
+        turn(1, both)
+        group_h(1, both, act)
+        for i in both:
+            for s in range(PASSES):
+                layer1(2, i, s)
+            activate(2, i)
+        add_shared(0)
+        scatter(0, (0, 1))
+        quantize_h(1, both)
+        layer2(1, 0)
+        layer2(1, 1)
+        scatter(0, (2,))
+        turn(2, both)
+        group_h(2, both, act)
+        for i in both:
+            for s in range(PASSES):
+                layer1(3, i, s)
+            activate(3, i)
+        gate_y(1)
+        for c in (1, 2, 3):
+            if c + 1 < E:
+                quantize_h(c + 1, both)
+            add_shared(c)
+            if c + 1 < E:
+                layer2(c + 1, 0)
+                layer2(c + 1, 1)
+                gate_y(c + 1)
+            if c + 2 < E:
+                turn(c + 2, both)
+                group_h(c + 2, both, act)
+            scatter(c, range(NB))

@@ -10,7 +10,9 @@ P = 128
 SHARED = E
 PASSES = K // 512
 NB = N // P
-ON_GPSIMD = (1, 2, 3,)
+ORDER = (3, 2, 0, 1)
+LAST = E - 1
+CAST_SPLIT = 320
 
 F32 = mybir.dt.float32
 BF16 = mybir.dt.bfloat16
@@ -22,6 +24,7 @@ FP8X4 = mybir.dt.float8_e4m3fn_x4
 FP4X4 = mybir.dt.float4_e2m1fn_x4
 ADD = mybir.AluOpType.add
 MULT = mybir.AluOpType.mult
+COPY = mybir.ActivationFunctionType.Copy
 GELU = mybir.ActivationFunctionType.Gelu_apprx_tanh
 
 
@@ -31,276 +34,321 @@ def tile_moe_shr_mlp_gelu_kernel(
     nc = tc.nc
     with ExitStack() as ctx:
         keep = ctx.enter_context(tc.tile_pool(name="keep", bufs=1))
-        work = ctx.enter_context(tc.tile_pool(name="work", bufs=2))
         ps_l1 = ctx.enter_context(tc.psum_pool(name="ps_l1", bufs=4))
         ps_t = ctx.enter_context(tc.psum_pool(name="ps_t", bufs=2))
         ps_y = ctx.enter_context(tc.psum_pool(name="ps_y", bufs=1))
 
         offsets = keep.tile([P, E * C // 16], U16, name="offsets")
-        w1_planes = keep.tile([P, (E + 1) * PASSES, H], U8, name="w1_planes", align_bytes=64)
-        w2_planes = keep.tile([P, E + 1, N], U8, name="w2_planes", align_bytes=64)
-        w2_t = keep.tile([P, E + 1, 2 * N], U8, name="w2_t", align_bytes=64)
-        w1_t = keep.tile([P, E + 1, PASSES, 2 * H], U8, name="w1_t", align_bytes=64)
-        gate_t = keep.tile([P, NB, E * C], F32, name="gate_t")
+        sc1_a = keep.tile([P, 3 * PASSES, H], U8, name="sc1_a", align_bytes=64)
+        sc2 = keep.tile([P, E + 1, N], U8, name="sc2", align_bytes=64)
+        w1_a = [keep.tile([P, 2, 2 * H], U8, name=f"w1_a{s}", align_bytes=64) for s in range(PASSES)]
+        w1_b = [keep.tile([P, PASSES, 2 * H], U8, name=f"w1_b{e}", align_bytes=64) for e in range(3)]
+        w2_a = keep.tile([P, 3, 2 * N], U8, name="w2_a", align_bytes=64)
+        w2_b = keep.tile([P, 2, 2 * N], U8, name="w2_b", align_bytes=64)
+        gate_t = keep.tile([P, 2 * C], F32, name="gate_t")
         ident = keep.tile([P, P], F32, name="ident")
         warm = keep.tile([P, 1], F32, name="warm")
         warm_out = keep.tile([P, 1], F32, name="warm_out")
-        raw_0 = keep.tile([P, 3, 2, T], F32, name="raw_0")
-        raw_1 = keep.tile([P, 3, 2, T], F32, name="raw_1")
-        raw = [raw_0[:, n] for n in range(3)] + [raw_1[:, n] for n in range(3)]
+        raw = [keep.tile([P, 2, T], F32, name=f"raw{n}", align_bytes=64) for n in range(2 * PASSES - 1)]
+        raw_5a = keep.tile([P, 2, T // 2], F32, name="raw_5a")
+        rest = keep.tile([P, 12 * C], U32, name="rest", align_bytes=64)
+        raw_end = [raw_5a[:], rest[:, 4 * C : 8 * C].bitcast(F32).rearrange("p (j t) -> p j t", j=2)]
         pairs = keep.tile([P, 2 * PASSES * T * 2], BF16, name="pairs", align_bytes=64)
-        planes = [keep.tile([P, 2, E * C, 2], BF16, name=f"planes{s}", align_bytes=64) for s in range(PASSES)]
-        slots = [keep.tile([P, E * C, 4], BF16, name=f"slots{s}", align_bytes=64) for s in range(PASSES)]
-        x_codes = [keep.tile([P, E * C], U32, name=f"x_codes{s}", align_bytes=64) for s in range(PASSES)]
-        x_scales = [keep.tile([P, E * C], U8, name=f"x_scales{s}", align_bytes=64) for s in range(PASSES)]
+        planes = keep.tile([P, 4 * T], U32, name="planes", align_bytes=64)
+        slots_first = keep.tile([P, 4 * C], U32, name="slots_first", align_bytes=64)
+        second = keep.tile([P, 6 * C], U32, name="second", align_bytes=64)
+        late = keep.tile([P, 6 * C], U32, name="late", align_bytes=64)
+        widths = (C, C, 2 * C)
+        x_codes = [keep.tile([P, PASSES * w], U32, name=f"x_codes{g}", align_bytes=64) for g, w in enumerate(widths)]
+        x_scales = [keep.tile([P, PASSES * w], U8, name=f"x_scales{g}", align_bytes=64) for g, w in enumerate(widths)]
         out_t = [keep.tile([P, T], F32, name=f"out_t{b}") for b in range(NB)]
+        h_act = [[keep.tile([P, H], BF16, name=f"h{u}{i}", align_bytes=64)[:] for i in range(2)] for u in range(E)]
+        h_rows = [keep.tile([P, 4 * C], U32, name=f"rows{u}", align_bytes=64) for u in range(E)]
+        h_codes = [keep.tile([P, 2 * C], U32, name=f"h_codes{u}", align_bytes=64) for u in range(E)]
+        h_scales = [keep.tile([P, 2 * C], U8, name=f"h_scales{u}", align_bytes=64) for u in range(E)]
+        gated = [keep.tile([P, N], F32, name=f"gated{u}")[:] for u in range(E)]
+        ys_rows = [keep.tile([P, N], F32, name=f"ys_rows{u}")[:] for u in range(E)]
+        by_slot = [keep.tile([P, N], F32, name=f"by_slot{e}") for e in range(2)]
+        gate_col = keep.tile([P, 2], F32, name="gate_col")
+        h_act[1][1] = ys_rows[0][:, C:].bitcast(BF16)
+        h_act[2][1] = ys_rows[1][:, C:].bitcast(BF16)
+        h_act[3][1] = gated[2][:, C:].bitcast(BF16)
 
-        nc.vector.memset(w1_planes[:, 0:10, :].rearrange("p a i -> p (a i)").bitcast(I32), 0)
-        nc.gpsimd.memset(w1_planes[:, 10:15, :].rearrange("p a i -> p (a i)").bitcast(I32), 0)
-        nc.vector.memset(raw_1[:, :, 0, 0:1], 0.0)
-        nc.vector.memset(w1_t[:].bitcast(I32)[:, :, 0, 0:1], 0)
-        nc.vector.memset(w2_t[:].bitcast(I32)[:, :, 0:1], 0)
-        nc.vector.memset(gate_t[:, :, 0:1], 0.0)
-        nc.gpsimd.memset(w2_planes[:].rearrange("p a i -> p (a i)").bitcast(I32), 0)
+        def words(tile):
+            return tile[:].rearrange("p a i -> p (a i)").bitcast(I32)
+
+        nc.gpsimd.memset(words(sc2), 0)
         make_identity(nc, ident[:])
         nc.vector.memset(warm[:], 0.0)
         nc.scalar.activation(warm_out[:], warm[:], GELU)
+        nc.vector.memset(words(sc1_a), 0)
 
-        x_rows = xT.rearrange("(s p u j) t -> s u p (j t)", s=PASSES, p=P, u=2)
-        w1_src = w1_words.bitcast(I32).rearrange("e s p b -> e p s b")
-
-        def load_x(n):
-            nc.sync.dma_start(raw[n].rearrange("p j t -> p (j t)"), x_rows[n // 2, n % 2])
-
-        def load_w1(e):
-            nc.sync.dma_start(w1_t[:, e].bitcast(I32), w1_src[e])
-
+        x_rows = xT.rearrange("(s p u j) t -> s u p j t", s=PASSES, p=P, u=2)
+        w1_src = w1_words.bitcast(I32)
+        w2_src = w2_words.bitcast(I32).rearrange("e a p b -> p (e a) b")
         w1_sc = w1_scales.bitcast(I32).rearrange("e s (a r) i -> r a (e s) i", r=4)
         w2_sc = w2_scales.bitcast(I32).rearrange("e s (a r) i -> r a (e s) i", r=4)
 
+        def load_x(n):
+            nc.sync.dma_start(raw[n][:], x_rows[n // 2, n % 2])
+
+        def load_scales(dst, src, queue):
+            for r in range(4):
+                queue.dma_start(dst[r:P:32].bitcast(I32), src[r])
+
+        def load_w1_a(s):
+            nc.sync.dma_start(w1_a[s][:].bitcast(I32), w1_src[3:5, s].rearrange("e p b -> p e b"))
+
+        def load_w1_b(e):
+            nc.sync.dma_start(w1_b[e][:].bitcast(I32), w1_src[e].rearrange("s p b -> p s b"))
+
         load_x(0)
         nc.sync.dma_start(offsets[:], offs)
-        load_x(1)
-        load_x(2)
-        for r in range(4):
-            nc.sync.dma_start(w1_planes[r:P:32].bitcast(I32), w1_sc[r])
-        load_x(3)
-        load_x(4)
-        load_w1(SHARED)
-        load_x(5)
-        load_w1(0)
-        load_w1(1)
-        nc.sync.dma_start(w2_t[:].bitcast(I32), w2_words.bitcast(I32).rearrange("e a p b -> p (e a) b"))
-        nc.sync.dma_start(gate_t[:], gate.rearrange("(b p) j -> p b j", p=P))
-        load_w1(2)
-        load_w1(3)
+        for n in range(1, 5):
+            load_x(n)
+        load_scales(sc1_a, w1_sc[:, :, 2 * PASSES :], nc.sync)
+        load_w1_a(0)
+        for j in range(2):
+            nc.sync.dma_start(raw_end[j], x_rows[2, 1][:, :, j * T // 2 : (j + 1) * T // 2])
+        load_w1_a(1)
+        load_w1_a(2)
+        load_w1_b(2)
+        nc.sync.dma_start(w2_a[:].bitcast(I32), w2_src[:, 2:5])
+        load_w1_b(0)
+        nc.sync.dma_start(gate_t[:], gate[0:P, 2 * C :])
+        with nc.allow_non_contiguous_dma(reason="one gate value a partition"):
+            nc.sync.dma_start(gate_col[:], gate[0, : 2 * C].rearrange("(e p) -> p e", p=P))
+        load_w1_b(1)
+        nc.sync.dma_start(w2_b[:].bitcast(I32), w2_src[:, 0:2])
+        load_scales(sc2, w2_sc, nc.gpsimd)
 
-        for r in range(4):
-            nc.gpsimd.dma_start(w2_planes[r:P:32].bitcast(I32), w2_sc[r])
+        def w1_of(e, s):
+            scale = sc1_a[:, (e - 2) * PASSES + s, :] if e >= 2 else sc1_b[:, e * PASSES + s, :]
+            return (w1_a[s][:, e - 3, :] if e >= 3 else w1_b[e][:, s, :]), scale
+
+        def w2_of(e):
+            return w2_a[:, e - 2, :] if e >= 2 else w2_b[:, e, :]
 
         def block(n):
             return (2 * PASSES - 1 - n) * T
 
-        def cast(n, copy):
-            dst = pairs[:, 2 * block(n) : 2 * (block(n) + T)].rearrange("p (t j) -> p t j", j=2)
-            copy(dst, raw[n].rearrange("p j t -> p t j"))
+        def cast(n, src, lo, hi, copy):
+            dst = pairs[:, 2 * (block(n) + lo) : 2 * (block(n) + hi)].rearrange("p (t j) -> p t j", j=2)
+            copy(dst, src.rearrange("p j t -> p t j"))
 
-        def gather(n, lo, hi):
-            width = T if n == 0 else 2 * T
+        def gather(n, lo, hi, dst):
+            width = T if hi - lo < T else 2 * T
             window = pairs[:, 2 * block(n) : 2 * (block(n) + width)].bitcast(U32)
-            dst = planes[n // 2][:, n % 2, lo:hi, :].rearrange("p a e -> p (a e)").bitcast(U32)
             nc.vector.tensor_copy(dst, window.indirect(offsets[:, lo // 16 : hi // 16]))
 
-        def interleave(s, lo, hi, copy):
-            src = planes[s][:, :, lo:hi, :].bitcast(F32)[:, :, :, 0].rearrange("p u a -> p a u")
-            copy(slots[s][:, lo:hi, :].bitcast(F32), src)
+        def interleave(dst, src, count, copy):
+            two = src.bitcast(F32).rearrange("p (u a) -> p a u", u=2)[:, 0:count, :]
+            copy(dst.bitcast(F32).rearrange("p (a u) -> p a u", u=2), two)
 
-        def quantize_x(s, lo, hi):
+        def quantize_x(g, s_lo, s_hi, src):
+            cols = slice(s_lo * widths[g], s_hi * widths[g])
             nc.vector.quantize_mx(
-                out=x_codes[s][:, lo:hi].bitcast(FP8X4),
-                scales=x_scales[s][:, lo:hi],
-                in_=slots[s][:, lo:hi, :].rearrange("p a d -> p (a d)"),
+                out=x_codes[g][:, cols].bitcast(FP8X4), scales=x_scales[g][:, cols], in_=src.bitcast(BF16)
             )
+
+        def interleave_early(dst, s_lo, s_hi, lo, hi, copy):
+            src = planes[:].bitcast(F32).rearrange("p (s u a) -> p s a u", s=2, u=2)[:, s_lo:s_hi, lo:hi, :]
+            copy(dst.bitcast(F32).rearrange("p (s a u) -> p s a u", s=s_hi - s_lo, u=2), src)
 
         acc = {}
 
-        def layer1(c, i, s):
+        def layer1(u, i, s):
             if s == 0:
                 tile = ps_l1.tile([P, H], F32, name="acc")
-                acc[c, i] = tile
-            e = (c, SHARED)[i]
-            cols = slice(c * C, (c + 1) * C)
+                acc[u, i] = tile
+            w, w_scale = w1_of((ORDER[u], SHARED)[i], s)
+            g = min(u, 2)
+            lo = s * widths[g] + (u - g) * C
+            cols = slice(lo, lo + C)
             nc.tensor.matmul_mx(
-                out=acc[c, i][:],
-                lhsT=x_codes[s][:, cols].bitcast(FP8X4),
-                lhsT_scale=x_scales[s][:, cols],
-                rhs=w1_t[:, e, s, :].bitcast(FP4X4),
-                rhs_scale=w1_planes[:, e * PASSES + s, :],
+                out=acc[u, i][:],
+                lhsT=x_codes[g][:, cols].bitcast(FP8X4),
+                lhsT_scale=x_scales[g][:, cols],
+                rhs=w.bitcast(FP4X4),
+                rhs_scale=w_scale,
                 start=(s == 0),
                 stop=(s == PASSES - 1),
             )
 
-        h_act = {}
+        def activate(u, i):
+            src = acc[u, i][:].rearrange("p (m v d) -> p v m d", v=2, d=2)
+            nc.scalar.activation(h_act[u][i].rearrange("p (v m d) -> p v m d", v=2, d=2), src, GELU)
 
-        def activate(c, i):
-            h = work.tile([P, H], BF16, name=f"h{i}", align_bytes=64)
-            h_act[c, i] = h
-            nc.scalar.activation(h[:], acc[c, i][:], GELU)
+        def rows_of(u, lo, hi):
+            return h_rows[u][:, 2 * C * lo : 2 * C * hi]
 
-        h_rows, h_q, turned = {}, {}, {}
-
-        def turn(c, halves):
+        def turn(u, halves, copy):
             bank = ps_t.tile([P, 4, C], F32, name="bank")
             for i in halves:
-                turned[c, i] = bank
-                words = h_act[c, i][:].bitcast(F32)
-                for u in range(2):
-                    nc.tensor.transpose(bank[:, 2 * i + u, :], words[:, u : H // 2 : 2], ident[:])
-
-        def group_h(c, halves, copy):
-            if c not in h_rows:
-                rows = work.tile([P, 2, C, 4], BF16, name="rows", align_bytes=64)
-                h_rows[c] = rows
+                h_words = h_act[u][i].bitcast(F32)
+                for v in range(2):
+                    nc.tensor.transpose(bank[:, 2 * i + v, :], h_words[:, v * P : (v + 1) * P], ident[:])
             lo, hi = halves[0], halves[-1] + 1
-            src = turned[c, lo][:, 2 * lo : 2 * hi, :].rearrange("p (i u) r -> p i r u", u=2)
-            copy(h_rows[c][:, lo:hi].bitcast(F32), src)
+            src = bank[:, 2 * lo : 2 * hi, :].rearrange("p (i v) r -> p i r v", v=2)
+            dst = rows_of(u, lo, hi).bitcast(F32).rearrange("p (i r v) -> p i r v", r=C, v=2)
+            copy(dst, src)
 
-        def quantize_h(c, halves):
-            if c not in h_q:
-                h_codes = work.tile([P, 2 * C], U32, name="h_codes", align_bytes=64)
-                h_scales = work.tile([P, 2 * C], U8, name="h_scales", align_bytes=64)
-                h_q[c] = (h_codes, h_scales)
+        def quantize_h(u, halves):
             lo, hi = halves[0], halves[-1] + 1
             nc.vector.quantize_mx(
-                out=h_q[c][0][:, lo * C : hi * C].bitcast(FP8X4),
-                scales=h_q[c][1][:, lo * C : hi * C],
-                in_=h_rows[c][:, lo:hi].rearrange("p i r d -> p (i r d)"),
+                out=h_codes[u][:, lo * C : hi * C].bitcast(FP8X4),
+                scales=h_scales[u][:, lo * C : hi * C],
+                in_=rows_of(u, lo, hi).bitcast(BF16),
             )
 
-        y = {}
+        def layer2(dst, u, i, b):
+            e = (ORDER[u], SHARED)[i]
+            nc.tensor.matmul_mx(
+                out=dst,
+                lhsT=w2_of(e)[:, 2 * P * b : 2 * P * (b + 1)].bitcast(FP4X4),
+                lhsT_scale=sc2[:, e, P * b : P * (b + 1)],
+                rhs=h_codes[u][:, i * C : (i + 1) * C].bitcast(FP8X4),
+                rhs_scale=h_scales[u][:, i * C : (i + 1) * C],
+                start=True,
+                stop=True,
+            )
 
-        def layer2(c, i):
-            y_i = ps_y.tile([P, NB, C], F32, name=f"y{i}")
-            y[c, i] = y_i
-            e = (c, SHARED)[i]
+        def routed(u):
+            y = ps_y.tile([P, NB, C], F32, name="y")
             for b in range(NB):
+                layer2(y[:, b, :], u, 0, b)
+            gate_u = gate_t[:, (ORDER[u] - 2) * C : (ORDER[u] - 1) * C].unsqueeze(1).to_broadcast([P, NB, C])
+            nc.vector.tensor_tensor(gated[u].rearrange("p (b c) -> p b c", c=C), y[:], gate_u, MULT)
+
+        def routed_by_slot(u):
+            e = ORDER[u]
+            y = ps_y.tile([P, N], F32, name="y")
+            for lo, hi in ((0, 2 * P), (2 * P, N)):
                 nc.tensor.matmul_mx(
-                    out=y_i[:, b, :],
-                    lhsT=w2_t[:, e, 2 * P * b : 2 * P * (b + 1)].bitcast(FP4X4),
-                    lhsT_scale=w2_planes[:, e, P * b : P * (b + 1)],
-                    rhs=h_q[c][0][:, i * C : (i + 1) * C].bitcast(FP8X4),
-                    rhs_scale=h_q[c][1][:, i * C : (i + 1) * C],
+                    out=y[:, lo:hi],
+                    lhsT=h_codes[u][:, :C].bitcast(FP8X4),
+                    lhsT_scale=h_scales[u][:, :C],
+                    rhs=w2_of(e)[:, 2 * lo : 2 * hi].bitcast(FP4X4),
+                    rhs_scale=sc2[:, e, lo:hi],
                     start=True,
                     stop=True,
                 )
+            nc.scalar.activation(by_slot[e][:], y[:], COPY, scale=gate_col[:, e : e + 1])
 
-        gated, summed = {}, {}
+        def turn_back(u):
+            y = ps_y.tile([P, N], F32, name="y")
+            for b in range(NB):
+                nc.tensor.transpose(y[:, b * P : (b + 1) * P], by_slot[ORDER[u]][:, b * P : (b + 1) * P], ident[:])
+            nc.scalar.copy(gated[u], y[:])
 
-        def gate_y(c):
-            gated_c = work.tile([P, NB, C], F32, name="gated_c")
-            gated[c] = gated_c
-            gate_c = gate_t[:, :, c * C : (c + 1) * C]
-            if c in ON_GPSIMD:
-                y_rows = work.tile([P, NB, C], F32, name="y_rows")
-                nc.scalar.copy(y_rows[:], y[c, 0][:])
-                nc.gpsimd.tensor_tensor(gated_c[:], y_rows[:], gate_c, MULT)
-            else:
-                nc.vector.tensor_tensor(gated_c[:], y[c, 0][:], gate_c, MULT)
+        ys_bank = {}
 
-        def add_shared(c):
-            total = work.tile([P, NB, C], F32, name="total")
-            summed[c] = total
-            nc.vector.tensor_tensor(total[:], y[c, 1][:], gated[c][:], ADD)
+        def shared(u, blocks):
+            ys = ps_y.tile([P, 4 * C], F32, name="ys")
+            ys_bank[u] = ys
+            for j, (v, b) in enumerate(blocks):
+                layer2(ys[:, j * C : (j + 1) * C], v, 1, b)
 
-        def scatter(c, blocks):
-            for b in blocks:
-                where = offsets[:, c * C // 16 : (c + 1) * C // 16]
-                nc.vector.tensor_copy(out_t[b][:].indirect(where), summed[c][:, b, :])
-                if c == E - 1:
-                    nc.sync.dma_start(out[b * P : (b + 1) * P, :], out_t[b][:])
+        def ys_of(u, b):
+            return ys_rows[u][:, b * C : (b + 1) * C]
+
+        def shared_out(u, at, v, lo, hi):
+            nc.scalar.copy(ys_rows[v][:, lo * C : hi * C], ys_bank[u][:, at * C : (at + hi - lo) * C])
+
+        def scatter(u, b):
+            where = offsets[:, ORDER[u] * C // 16 : (ORDER[u] + 1) * C // 16]
+            nc.vector.tensor_tensor(out_t[b][:].indirect(where), gated[u][:, b * C : (b + 1) * C], ys_of(u, b), ADD)
+            if u == LAST:
+                nc.sync.dma_start(out[b * P : (b + 1) * P, :], out_t[b][:])
 
         vec, act = nc.vector.tensor_copy, nc.scalar.copy
         both = (0, 1)
+        first = 3 * C
 
-        cast(0, vec)
-        gather(0, 0, 256)
-        gather(0, 256, 512)
-        cast(1, act)
-        gather(1, 0, 512)
-        cast(2, act)
-        cast(3, act)
-        interleave(0, 0, 512, act)
-        gather(2, 0, 512)
-        gather(3, 0, 512)
-        quantize_x(0, 0, 512)
-        for i in both:
-            layer1(0, i, 0)
-        cast(4, act)
-        gather(4, 0, 128)
-        interleave(1, 0, 512, vec)
-        cast(5, act)
-        quantize_x(1, 0, 512)
-        for i in both:
-            layer1(0, i, 1)
-        gather(5, 0, 128)
-        gather(4, 128, 256)
-        interleave(2, 0, 128, vec)
-        gather(5, 128, 256)
-        quantize_x(2, 0, 128)
-        for i in both:
-            layer1(1, i, 0)
+        def gather_at_step(n, lo, hi, dst):
+            gather(n, lo, hi, dst.rearrange("p (a u) -> p a u", u=2)[:, :, n % 2])
+
+        cast(0, raw[0][:, :, :CAST_SPLIT], 0, CAST_SPLIT, vec)
+        cast(0, raw[0][:, :, CAST_SPLIT:], CAST_SPLIT, T, act)
+        for n in range(1, 5):
+            cast(n, raw[n][:], 0, T, act)
+        sc1_b = keep.tile([P, 2 * PASSES, H], U8, name="sc1_b", tag="raw4", align_bytes=64)
+        nc.gpsimd.memset(words(sc1_b), 0)
+        load_scales(sc1_b, w1_sc[:, :, : 2 * PASSES], nc.gpsimd)
+        for j in range(2):
+            cast(5, raw_end[j], j * T // 2, (j + 1) * T // 2, act)
+        gather(0, 0, first, planes[:, :first])
+        gather(0, first, T, planes[:, first:T])
+        for n in range(1, 4):
+            gather(n, 0, T, planes[:, n * T : (n + 1) * T])
+        interleave_early(slots_first[:, : 4 * C], 0, 2, first, T, act)
+        interleave_early(second[:, : 4 * C], 0, 2, 2 * C, first, act)
+        gather_at_step(4, first, T, late[:, 3 * C : 5 * C])
+        quantize_x(0, 0, 2, slots_first[:, : 4 * C])
+        for s in range(2):
+            for i in both:
+                layer1(0, i, s)
+        gather_at_step(4, 2 * C, first, second[:, 4 * C :])
+        gather(4, 0, 2 * C, late[:, : 2 * C])
+        quantize_x(1, 0, 2, second[:, : 4 * C])
+        gather_at_step(5, first, T, late[:, 3 * C : 5 * C])
+        gather_at_step(5, 2 * C, first, second[:, 4 * C :])
+        quantize_x(0, 2, 3, late[:, 3 * C : 5 * C])
         for i in both:
             layer1(0, i, 2)
             activate(0, i)
-        interleave(2, 128, 256, vec)
-        gather(4, 256, 512)
-        quantize_x(2, 128, 256)
-        for i in both:
-            layer1(1, i, 1)
-        turn(0, (0,))
-        for i in both:
-            layer1(1, i, 2)
-        turn(0, (1,))
-        group_h(0, (0,), vec)
-        group_h(0, (1,), act)
-        gather(5, 256, 512)
+        interleave_early(rest[:, : 8 * C], 0, 2, 0, 2 * C, act)
+        quantize_x(1, 2, 3, second[:, 4 * C :])
+        gather(5, 0, 2 * C, late[:, 3 * C : 5 * C])
+        quantize_x(2, 0, 2, rest[:, : 8 * C])
+        interleave(rest[:, 8 * C :], late[:], 2 * C, vec)
+        turn(0, (0,), vec)
         quantize_h(0, (0,))
-        interleave(2, 256, 512, vec)
-        layer2(0, 0)
+        turn(0, (1,), act)
+        quantize_h(0, (1,))
+        quantize_x(2, 2, 3, rest[:, 8 * C :])
+        routed(0)
+        shared(0, [(0, 0), (0, 1)])
+        shared_out(0, 0, 0, 0, 1)
+        scatter(0, 0)
+        for s in range(PASSES):
+            for i in both:
+                layer1(1, i, s)
         for i in both:
             activate(1, i)
-        quantize_h(0, (1,))
-        layer2(0, 1)
-        quantize_x(2, 256, 512)
-        gate_y(0)
-        turn(1, both)
-        group_h(1, both, act)
-        for i in both:
-            for s in range(PASSES):
-                layer1(2, i, s)
-            activate(2, i)
-        add_shared(0)
-        scatter(0, (0, 1))
+
+        def first_layer(u):
+            for i in both:
+                for s in range(PASSES):
+                    layer1(u, i, s)
+                activate(u, i)
+
+        turn(1, both, act)
         quantize_h(1, both)
-        layer2(1, 0)
-        layer2(1, 1)
-        scatter(0, (2,))
-        turn(2, both)
-        group_h(2, both, act)
-        for i in both:
-            for s in range(PASSES):
-                layer1(3, i, s)
-            activate(3, i)
-        gate_y(1)
-        for c in (1, 2, 3):
-            if c + 1 < E:
-                quantize_h(c + 1, both)
-            add_shared(c)
-            if c + 1 < E:
-                layer2(c + 1, 0)
-                layer2(c + 1, 1)
-                gate_y(c + 1)
-            if c + 2 < E:
-                turn(c + 2, both)
-                group_h(c + 2, both, act)
-            scatter(c, range(NB))
+        shared_out(0, 1, 0, 1, 2)
+        scatter(0, 1)
+        routed(1)
+        shared(1, [(0, 2), (1, 0), (1, 1), (1, 2)])
+        shared_out(1, 0, 0, 2, 3)
+        scatter(0, 2)
+        first_layer(2)
+        turn(2, both, act)
+        quantize_h(2, both)
+        shared_out(1, 1, 1, 0, NB)
+        for b in range(NB):
+            scatter(1, b)
+        routed_by_slot(2)
+        shared(2, [(2, b) for b in range(NB)])
+        shared_out(2, 0, 2, 0, NB)
+        first_layer(3)
+        turn(3, both, act)
+        quantize_h(3, both)
+        turn_back(2)
+        for b in range(NB):
+            scatter(2, b)
+        routed_by_slot(3)
+        shared(3, [(3, b) for b in range(NB)])
+        shared_out(3, 0, 3, 0, NB)
+        turn_back(3)
+        for b in range(NB):
+            scatter(3, b)

@@ -50,14 +50,14 @@ def tile_moe_shr_mlp_gelu_kernel(
         warm = keep.tile([P, 1], F32, name="warm")
         warm_out = keep.tile([P, 1], F32, name="warm_out")
         raw = [keep.tile([P, 2, T], F32, name=f"raw{n}", align_bytes=64) for n in range(2 * PASSES - 1)]
-        raw_5a = keep.tile([P, 2, T // 2], F32, name="raw_5a")
+        raw_5a = keep.tile([P, 2, T // 2], F32, name="raw_5a", align_bytes=64)
         rest = keep.tile([P, 12 * C], U32, name="rest", align_bytes=64)
         raw_end = [raw_5a[:], rest[:, 4 * C : 8 * C].bitcast(F32).rearrange("p (j t) -> p j t", j=2)]
         pairs = keep.tile([P, 2 * PASSES * T * 2], BF16, name="pairs", align_bytes=64)
         planes = keep.tile([P, 4 * T], U32, name="planes", align_bytes=64)
-        slots_first = keep.tile([P, 4 * C], U32, name="slots_first", align_bytes=64)
-        second = keep.tile([P, 6 * C], U32, name="second", align_bytes=64)
-        late = keep.tile([P, 6 * C], U32, name="late", align_bytes=64)
+        slots_first = raw[4][:, 0, :].bitcast(U32)
+        second = raw_5a[:].rearrange("p j t -> p (j t)").bitcast(U32)
+        late = keep.tile([P, 2 * C], U32, name="late", align_bytes=64)
         widths = (C, C, 2 * C)
         x_codes = [keep.tile([P, PASSES * w], U32, name=f"x_codes{g}", align_bytes=64) for g, w in enumerate(widths)]
         x_scales = [keep.tile([P, PASSES * w], U8, name=f"x_scales{g}", align_bytes=64) for g, w in enumerate(widths)]
@@ -114,8 +114,8 @@ def tile_moe_shr_mlp_gelu_kernel(
         load_w1_a(2)
         load_w1_b(2)
         nc.sync.dma_start(w2_a[:].bitcast(I32), w2_src[:, 2:5])
-        load_w1_b(0)
         nc.sync.dma_start(gate_t[:], gate[0:P, 2 * C :])
+        load_w1_b(0)
         with nc.allow_non_contiguous_dma(reason="one gate value a partition"):
             nc.sync.dma_start(gate_col[:], gate[0, : 2 * C].rearrange("(e p) -> p e", p=P))
         load_w1_b(1)
@@ -137,12 +137,11 @@ def tile_moe_shr_mlp_gelu_kernel(
             copy(dst, src.rearrange("p j t -> p t j"))
 
         def gather(n, lo, hi, dst):
-            width = T if hi - lo < T else 2 * T
-            window = pairs[:, 2 * block(n) : 2 * (block(n) + width)].bitcast(U32)
+            window = pairs[:, 2 * block(n) : 2 * (block(n) + T)].bitcast(U32)
             nc.vector.tensor_copy(dst, window.indirect(offsets[:, lo // 16 : hi // 16]))
 
-        def interleave(dst, src, count, copy):
-            two = src.bitcast(F32).rearrange("p (u a) -> p a u", u=2)[:, 0:count, :]
+        def interleave(dst, src, copy):
+            two = src.bitcast(F32).rearrange("p (u a) -> p a u", u=2)
             copy(dst.bitcast(F32).rearrange("p (a u) -> p a u", u=2), two)
 
         def quantize_x(g, s_lo, s_hi, src):
@@ -151,9 +150,9 @@ def tile_moe_shr_mlp_gelu_kernel(
                 out=x_codes[g][:, cols].bitcast(FP8X4), scales=x_scales[g][:, cols], in_=src.bitcast(BF16)
             )
 
-        def interleave_early(dst, s_lo, s_hi, lo, hi, copy):
-            src = planes[:].bitcast(F32).rearrange("p (s u a) -> p s a u", s=2, u=2)[:, s_lo:s_hi, lo:hi, :]
-            copy(dst.bitcast(F32).rearrange("p (s a u) -> p s a u", s=s_hi - s_lo, u=2), src)
+        def interleave_early(dst, part, lo, hi, copy):
+            src = part.bitcast(F32).rearrange("p (s u a) -> p s a u", s=2, u=2)[:, :, lo:hi, :]
+            copy(dst.bitcast(F32).rearrange("p (s a u) -> p s a u", s=2, u=2), src)
 
         acc = {}
 
@@ -272,49 +271,48 @@ def tile_moe_shr_mlp_gelu_kernel(
         cast(0, raw[0][:, :, CAST_SPLIT:], CAST_SPLIT, T, act)
         for n in range(1, 5):
             cast(n, raw[n][:], 0, T, act)
-        sc1_b = keep.tile([P, 2 * PASSES, H], U8, name="sc1_b", tag="raw4", align_bytes=64)
+        sc1_b = keep.tile([P, 2 * PASSES, H], U8, name="sc1_b", tag="raw3", align_bytes=64)
         nc.gpsimd.memset(words(sc1_b), 0)
         load_scales(sc1_b, w1_sc[:, :, : 2 * PASSES], nc.gpsimd)
+        planes_first, planes_rest = planes[:, : 4 * C], planes[:, 4 * C :]
+        for n in range(4):
+            gather(n, first, T, planes_first[:, n * C : (n + 1) * C])
+            gather(n, 0, first, planes_rest[:, n * first : (n + 1) * first])
+        interleave_early(slots_first, planes_first, 0, C, act)
         for j in range(2):
             cast(5, raw_end[j], j * T // 2, (j + 1) * T // 2, act)
-        gather(0, 0, first, planes[:, :first])
-        gather(0, first, T, planes[:, first:T])
-        for n in range(1, 4):
-            gather(n, 0, T, planes[:, n * T : (n + 1) * T])
-        interleave_early(slots_first[:, : 4 * C], 0, 2, first, T, act)
-        interleave_early(second[:, : 4 * C], 0, 2, 2 * C, first, act)
-        gather_at_step(4, first, T, late[:, 3 * C : 5 * C])
-        quantize_x(0, 0, 2, slots_first[:, : 4 * C])
+        interleave_early(second, planes_rest, 2 * C, first, act)
+        interleave_early(rest[:, : 8 * C], planes_rest, 0, 2 * C, act)
+        gather_at_step(4, first, T, late[:])
+        quantize_x(0, 0, 2, slots_first)
         for s in range(2):
             for i in both:
                 layer1(0, i, s)
-        gather_at_step(4, 2 * C, first, second[:, 4 * C :])
-        gather(4, 0, 2 * C, late[:, : 2 * C])
-        quantize_x(1, 0, 2, second[:, : 4 * C])
-        gather_at_step(5, first, T, late[:, 3 * C : 5 * C])
-        gather_at_step(5, 2 * C, first, second[:, 4 * C :])
-        quantize_x(0, 2, 3, late[:, 3 * C : 5 * C])
+        gather_at_step(4, 2 * C, first, planes[:, : 2 * C])
+        gather(4, 0, 2 * C, planes[:, 2 * C : 4 * C])
+        gather_at_step(5, first, T, late[:])
+        gather_at_step(5, 2 * C, first, planes[:, : 2 * C])
+        quantize_x(0, 2, 3, late[:])
         for i in both:
             layer1(0, i, 2)
             activate(0, i)
-        interleave_early(rest[:, : 8 * C], 0, 2, 0, 2 * C, act)
-        quantize_x(1, 2, 3, second[:, 4 * C :])
-        gather(5, 0, 2 * C, late[:, 3 * C : 5 * C])
+        quantize_x(1, 0, 2, second)
+        quantize_x(1, 2, 3, planes[:, : 2 * C])
+        gather(5, 0, 2 * C, planes[:, 4 * C : 6 * C])
         quantize_x(2, 0, 2, rest[:, : 8 * C])
-        interleave(rest[:, 8 * C :], late[:], 2 * C, vec)
         turn(0, (0,), vec)
         quantize_h(0, (0,))
         turn(0, (1,), act)
         quantize_h(0, (1,))
+        interleave(rest[:, 8 * C :], planes[:, 2 * C : 6 * C], vec)
         quantize_x(2, 2, 3, rest[:, 8 * C :])
         routed(0)
         shared(0, [(0, 0), (0, 1)])
         shared_out(0, 0, 0, 0, 1)
         scatter(0, 0)
-        for s in range(PASSES):
-            for i in both:
+        for i in (1, 0):
+            for s in range(PASSES):
                 layer1(1, i, s)
-        for i in both:
             activate(1, i)
 
         def first_layer(u):

@@ -54,15 +54,17 @@ def tile_moe_shr_mlp_gelu_kernel(
         rest = keep.tile([P, 12 * C], U32, name="rest", align_bytes=64)
         raw_end = [raw_5a[:], rest[:, 4 * C : 8 * C].bitcast(F32).rearrange("p (j t) -> p j t", j=2)]
         pairs = keep.tile([P, 2 * PASSES * T * 2], BF16, name="pairs", align_bytes=64)
-        planes = keep.tile([P, 4 * T], U32, name="planes", align_bytes=64)
-        slots_first = raw[4][:, 0, :].bitcast(U32)
+        planes = keep.tile([P, 18 * C], U32, name="planes", align_bytes=64)
+        slots_first = raw[4][:, 0, : 2 * C].bitcast(U32)
         second = raw_5a[:].rearrange("p j t -> p (j t)").bitcast(U32)
-        late = keep.tile([P, 2 * C], U32, name="late", align_bytes=64)
+        late, late_second = planes[:, : 2 * C], planes[:, 2 * C : 4 * C]
+        slots_zero = keep.tile([P, 2 * C], U32, name="slots_zero", align_bytes=64)
         widths = (C, C, 2 * C)
         x_codes = [keep.tile([P, PASSES * w], U32, name=f"x_codes{g}", align_bytes=64) for g, w in enumerate(widths)]
-        x_scales = [keep.tile([P, PASSES * w], U8, name=f"x_scales{g}", align_bytes=64) for g, w in enumerate(widths)]
+        x_scales = {g: keep.tile([P, PASSES * widths[g]], U8, name=f"x_scales{g}", align_bytes=64) for g in (1, 2)}
         out_t = [keep.tile([P, T], F32, name=f"out_t{b}") for b in range(NB)]
-        h_act = [[keep.tile([P, H], BF16, name=f"h{u}{i}", align_bytes=64)[:] for i in range(2)] for u in range(E)]
+        h_own = [keep.tile([P, H], BF16, name=f"h{j}", align_bytes=64)[:] for j in range(3)]
+        h_act = {0: {0: h_own[0], 1: h_own[1]}, 1: {}, 2: {}, 3: {0: h_own[2]}}
         h_rows = [keep.tile([P, 4 * C], U32, name=f"rows{u}", align_bytes=64) for u in range(E)]
         h_codes = [keep.tile([P, 2 * C], U32, name=f"h_codes{u}", align_bytes=64) for u in range(E)]
         h_scales = [keep.tile([P, 2 * C], U8, name=f"h_scales{u}", align_bytes=64) for u in range(E)]
@@ -71,8 +73,10 @@ def tile_moe_shr_mlp_gelu_kernel(
         by_slot = [keep.tile([P, N], F32, name=f"by_slot{e}") for e in range(2)]
         gate_col = keep.tile([P, 2], F32, name="gate_col")
         h_act[1][1] = ys_rows[0][:, C:].bitcast(BF16)
-        h_act[2][1] = ys_rows[1][:, C:].bitcast(BF16)
-        h_act[3][1] = gated[2][:, C:].bitcast(BF16)
+        h_act[1][0] = ys_rows[1][:, C:].bitcast(BF16)
+        h_act[2][1] = h_act[1][0]
+        h_act[2][0] = gated[2][:, C:].bitcast(BF16)
+        h_act[3][1] = h_act[2][0]
 
         def words(tile):
             return tile[:].rearrange("p a i -> p (a i)").bitcast(I32)
@@ -113,12 +117,12 @@ def tile_moe_shr_mlp_gelu_kernel(
         load_w1_a(1)
         load_w1_a(2)
         load_w1_b(2)
+        load_w1_b(0)
         nc.sync.dma_start(w2_a[:].bitcast(I32), w2_src[:, 2:5])
         nc.sync.dma_start(gate_t[:], gate[0:P, 2 * C :])
-        load_w1_b(0)
+        load_w1_b(1)
         with nc.allow_non_contiguous_dma(reason="one gate value a partition"):
             nc.sync.dma_start(gate_col[:], gate[0, : 2 * C].rearrange("(e p) -> p e", p=P))
-        load_w1_b(1)
         nc.sync.dma_start(w2_b[:].bitcast(I32), w2_src[:, 0:2])
         load_scales(sc2, w2_sc, nc.gpsimd)
 
@@ -274,71 +278,78 @@ def tile_moe_shr_mlp_gelu_kernel(
         sc1_b = keep.tile([P, 2 * PASSES, H], U8, name="sc1_b", tag="raw3", align_bytes=64)
         nc.gpsimd.memset(words(sc1_b), 0)
         load_scales(sc1_b, w1_sc[:, :, : 2 * PASSES], nc.gpsimd)
-        planes_first, planes_rest = planes[:, : 4 * C], planes[:, 4 * C :]
+        planes_first, planes_rest = planes[:, 2 * C : 6 * C], planes[:, 6 * C :]
+        x_scales[0] = keep.tile([P, PASSES * C], U8, name="x_scales0", tag="raw2", align_bytes=64)
         for n in range(4):
-            gather(n, first, T, planes_first[:, n * C : (n + 1) * C])
+            gather(n, first, T, planes_first[:, (n + 2) % 4 * C : ((n + 2) % 4 + 1) * C])
+            if n == 2:
+                quantize_x(0, 0, 1, slots_zero[:])
             gather(n, 0, first, planes_rest[:, n * first : (n + 1) * first])
-        interleave_early(slots_first, planes_first, 0, C, act)
+            if n == 1:
+                interleave(slots_zero[:], planes_first[:, 2 * C :], vec)
+        for i in both:
+            layer1(0, i, 0)
+        interleave(slots_first, planes_first[:, : 2 * C], act)
         for j in range(2):
             cast(5, raw_end[j], j * T // 2, (j + 1) * T // 2, act)
         interleave_early(second, planes_rest, 2 * C, first, act)
         interleave_early(rest[:, : 8 * C], planes_rest, 0, 2 * C, act)
-        gather_at_step(4, first, T, late[:])
-        quantize_x(0, 0, 2, slots_first)
-        for s in range(2):
-            for i in both:
-                layer1(0, i, s)
-        gather_at_step(4, 2 * C, first, planes[:, : 2 * C])
-        gather(4, 0, 2 * C, planes[:, 2 * C : 4 * C])
-        gather_at_step(5, first, T, late[:])
-        gather_at_step(5, 2 * C, first, planes[:, : 2 * C])
-        quantize_x(0, 2, 3, late[:])
+        gather_at_step(4, first, T, late)
+        quantize_x(0, 1, 2, slots_first)
+        for i in both:
+            layer1(0, i, 1)
+        gather_at_step(4, 2 * C, first, late_second)
+        gather_at_step(5, first, T, late)
+        gather_at_step(5, 2 * C, first, late_second)
+        quantize_x(0, 2, 3, late)
         for i in both:
             layer1(0, i, 2)
             activate(0, i)
         quantize_x(1, 0, 2, second)
-        quantize_x(1, 2, 3, planes[:, : 2 * C])
-        gather(5, 0, 2 * C, planes[:, 4 * C : 6 * C])
+        quantize_x(1, 2, 3, late_second)
+        gather(4, 0, 2 * C, late)
+        gather(5, 0, 2 * C, late_second)
         quantize_x(2, 0, 2, rest[:, : 8 * C])
         turn(0, (0,), vec)
         quantize_h(0, (0,))
-        turn(0, (1,), act)
+        turn(0, (1,), vec)
         quantize_h(0, (1,))
-        interleave(rest[:, 8 * C :], planes[:, 2 * C : 6 * C], vec)
+
+        def matmuls(u, i):
+            for s in range(PASSES):
+                layer1(u, i, s)
+
+        for i in (1, 0):
+            matmuls(1, i)
+            activate(1, i)
+        interleave(rest[:, 8 * C :], planes[:, : 4 * C], act)
         quantize_x(2, 2, 3, rest[:, 8 * C :])
         routed(0)
         shared(0, [(0, 0), (0, 1)])
         shared_out(0, 0, 0, 0, 1)
         scatter(0, 0)
-        for i in (1, 0):
-            for s in range(PASSES):
-                layer1(1, i, s)
-            activate(1, i)
-
-        def first_layer(u):
-            for i in both:
-                for s in range(PASSES):
-                    layer1(u, i, s)
-                activate(u, i)
-
         turn(1, both, act)
         quantize_h(1, both)
+        for i in (1, 0):
+            matmuls(2, i)
+            activate(2, i)
         shared_out(0, 1, 0, 1, 2)
         scatter(0, 1)
         routed(1)
         shared(1, [(0, 2), (1, 0), (1, 1), (1, 2)])
         shared_out(1, 0, 0, 2, 3)
         scatter(0, 2)
-        first_layer(2)
         turn(2, both, act)
         quantize_h(2, both)
         shared_out(1, 1, 1, 0, NB)
         for b in range(NB):
             scatter(1, b)
+        for i in both:
+            matmuls(3, i)
+            activate(3, i)
         routed_by_slot(2)
         shared(2, [(2, b) for b in range(NB)])
         shared_out(2, 0, 2, 0, NB)
-        first_layer(3)
         turn(3, both, act)
         quantize_h(3, both)
         turn_back(2)

@@ -40,8 +40,8 @@ def tile_moe_shr_mlp_gelu_kernel(
 
         offsets = keep.tile([P, E * C // 16], U16, name="offsets")
         sc1_a = keep.tile([P, 3 * PASSES, H], U8, name="sc1_a", align_bytes=64)
-        sc2 = keep.tile([P, E + 1, N], U8, name="sc2", align_bytes=64)
-        w1_a = [keep.tile([P, 2, 2 * H], U8, name=f"w1_a{s}", align_bytes=64) for s in range(PASSES)]
+        w1_a = [keep.tile([P, 2, 2 * H], U8, name=f"w1_a{s}", align_bytes=64) for s in range(PASSES - 1)]
+        w1_last = [keep.tile([P, 2 * H], U8, name=f"w1_last{j}", align_bytes=64) for j in range(2)]
         w1_b = [keep.tile([P, PASSES, 2 * H], U8, name=f"w1_b{e}", align_bytes=64) for e in range(3)]
         w2_a = keep.tile([P, 3, 2 * N], U8, name="w2_a", align_bytes=64)
         w2_b = keep.tile([P, 2, 2 * N], U8, name="w2_b", align_bytes=64)
@@ -81,7 +81,6 @@ def tile_moe_shr_mlp_gelu_kernel(
         def words(tile):
             return tile[:].rearrange("p a i -> p (a i)").bitcast(I32)
 
-        nc.gpsimd.memset(words(sc2), 0)
         make_identity(nc, ident[:])
         nc.vector.memset(warm[:], 0.0)
         nc.scalar.activation(warm_out[:], warm[:], GELU)
@@ -115,7 +114,8 @@ def tile_moe_shr_mlp_gelu_kernel(
         for j in range(2):
             nc.sync.dma_start(raw_end[j], x_rows[2, 1][:, :, j * T // 2 : (j + 1) * T // 2])
         load_w1_a(1)
-        load_w1_a(2)
+        for j in range(2):
+            nc.sync.dma_start(w1_last[j][:].bitcast(I32), w1_src[3 + j, PASSES - 1])
         load_w1_b(2)
         load_w1_b(0)
         nc.sync.dma_start(w2_a[:].bitcast(I32), w2_src[:, 2:5])
@@ -124,11 +124,12 @@ def tile_moe_shr_mlp_gelu_kernel(
         with nc.allow_non_contiguous_dma(reason="one gate value a partition"):
             nc.sync.dma_start(gate_col[:], gate[0, : 2 * C].rearrange("(e p) -> p e", p=P))
         nc.sync.dma_start(w2_b[:].bitcast(I32), w2_src[:, 0:2])
-        load_scales(sc2, w2_sc, nc.gpsimd)
 
         def w1_of(e, s):
             scale = sc1_a[:, (e - 2) * PASSES + s, :] if e >= 2 else sc1_b[:, e * PASSES + s, :]
-            return (w1_a[s][:, e - 3, :] if e >= 3 else w1_b[e][:, s, :]), scale
+            if e < 3:
+                return w1_b[e][:, s, :], scale
+            return (w1_a[s][:, e - 3, :] if s < PASSES - 1 else w1_last[e - 3][:]), scale
 
         def w2_of(e):
             return w2_a[:, e - 2, :] if e >= 2 else w2_b[:, e, :]
@@ -242,7 +243,8 @@ def tile_moe_shr_mlp_gelu_kernel(
             y = ps_y.tile([P, N], F32, name="y")
             for b in range(NB):
                 nc.tensor.transpose(y[:, b * P : (b + 1) * P], by_slot[ORDER[u]][:, b * P : (b + 1) * P], ident[:])
-            nc.scalar.copy(gated[u], y[:])
+            for lo, hi in ((0, P), (P, N)) if u == LAST else ((0, N),):
+                nc.scalar.copy(gated[u][:, lo:hi], y[:, lo:hi])
 
         ys_bank = {}
 
@@ -275,9 +277,9 @@ def tile_moe_shr_mlp_gelu_kernel(
         cast(0, raw[0][:, :, CAST_SPLIT:], CAST_SPLIT, T, act)
         for n in range(1, 5):
             cast(n, raw[n][:], 0, T, act)
-        sc1_b = keep.tile([P, 2 * PASSES, H], U8, name="sc1_b", tag="raw3", align_bytes=64)
-        nc.gpsimd.memset(words(sc1_b), 0)
-        load_scales(sc1_b, w1_sc[:, :, : 2 * PASSES], nc.gpsimd)
+        sc2 = keep.tile([P, E + 1, N], U8, name="sc2", tag="raw3", align_bytes=64)
+        nc.gpsimd.memset(words(sc2), 0)
+        load_scales(sc2, w2_sc, nc.gpsimd)
         planes_first, planes_rest = planes[:, 2 * C : 6 * C], planes[:, 6 * C :]
         x_scales[0] = keep.tile([P, PASSES * C], U8, name="x_scales0", tag="raw2", align_bytes=64)
         for n in range(4):
@@ -298,6 +300,9 @@ def tile_moe_shr_mlp_gelu_kernel(
         quantize_x(0, 1, 2, slots_first)
         for i in both:
             layer1(0, i, 1)
+        sc1_b = keep.tile([P, 2 * PASSES, H], U8, name="sc1_b", tag="raw4", align_bytes=64)
+        nc.gpsimd.memset(words(sc1_b), 0)
+        load_scales(sc1_b, w1_sc[:, :, : 2 * PASSES], nc.gpsimd)
         gather_at_step(4, 2 * C, first, late_second)
         gather_at_step(5, first, T, late)
         gather_at_step(5, 2 * C, first, late_second)

@@ -278,7 +278,6 @@ def tile_moe_shr_mlp_gelu_kernel(
         for n in range(1, 5):
             cast(n, raw[n][:], 0, T, act)
         sc2 = keep.tile([P, E + 1, N], U8, name="sc2", tag="raw3", align_bytes=64)
-        nc.gpsimd.memset(words(sc2), 0)
         load_scales(sc2, w2_sc, nc.gpsimd)
         planes_first, planes_rest = planes[:, 2 * C : 6 * C], planes[:, 6 * C :]
         x_scales[0] = keep.tile([P, PASSES * C], U8, name="x_scales0", tag="raw2", align_bytes=64)
@@ -301,7 +300,6 @@ def tile_moe_shr_mlp_gelu_kernel(
         for i in both:
             layer1(0, i, 1)
         sc1_b = keep.tile([P, 2 * PASSES, H], U8, name="sc1_b", tag="raw4", align_bytes=64)
-        nc.gpsimd.memset(words(sc1_b), 0)
         load_scales(sc1_b, w1_sc[:, :, : 2 * PASSES], nc.gpsimd)
         gather_at_step(4, 2 * C, first, late_second)
         gather_at_step(5, first, T, late)

@@ -13,6 +13,9 @@ NB = N // P
 ORDER = (3, 2, 0, 1)
 LAST = E - 1
 CAST_SPLIT = 320
+END_SPLIT = 160
+WIDE = 704
+ACC_BANK = {(0, 0): "a", (0, 1): "b", (1, 1): "c", (1, 0): "d", (2, 1): "d", (2, 0): "a", (3, 0): "b", (3, 1): "d"}
 
 F32 = mybir.dt.float32
 BF16 = mybir.dt.bfloat16
@@ -34,12 +37,13 @@ def tile_moe_shr_mlp_gelu_kernel(
     nc = tc.nc
     with ExitStack() as ctx:
         keep = ctx.enter_context(tc.tile_pool(name="keep", bufs=1))
-        ps_l1 = ctx.enter_context(tc.psum_pool(name="ps_l1", bufs=4))
+        ps_l1 = ctx.enter_context(tc.psum_pool(name="ps_l1", bufs=1))
         ps_t = ctx.enter_context(tc.psum_pool(name="ps_t", bufs=2))
         ps_y = ctx.enter_context(tc.psum_pool(name="ps_y", bufs=1))
 
         offsets = keep.tile([P, E * C // 16], U16, name="offsets")
-        sc1_a = keep.tile([P, 3 * PASSES, H], U8, name="sc1_a", align_bytes=64)
+        sc1_a = keep.tile([P, 2 * PASSES, H], U8, name="sc1_a", align_bytes=64)
+        sc1_c = keep.tile([P, PASSES, H], U8, name="sc1_c", align_bytes=64)
         w1_a = [keep.tile([P, 2, 2 * H], U8, name=f"w1_a{s}", align_bytes=64) for s in range(PASSES - 1)]
         w1_last = [keep.tile([P, 2 * H], U8, name=f"w1_last{j}", align_bytes=64) for j in range(2)]
         w1_b = [keep.tile([P, PASSES, 2 * H], U8, name=f"w1_b{e}", align_bytes=64) for e in range(3)]
@@ -49,24 +53,23 @@ def tile_moe_shr_mlp_gelu_kernel(
         ident = keep.tile([P, P], F32, name="ident")
         warm = keep.tile([P, 1], F32, name="warm")
         warm_out = keep.tile([P, 1], F32, name="warm_out")
-        raw = [keep.tile([P, 2, T], F32, name=f"raw{n}", align_bytes=64) for n in range(2 * PASSES - 1)]
-        raw_5a = keep.tile([P, 2, T // 2], F32, name="raw_5a", align_bytes=64)
+        raw = [keep.tile([P, 2, T], F32, name=f"raw{n}", align_bytes=64)[:] for n in range(2 * PASSES - 2)]
+        work = keep.tile([P, 3 * T], U32, name="work", align_bytes=64)
+        raw.append(work[:, : 2 * T].bitcast(F32).rearrange("p (j t) -> p j t", j=2))
+        raw_5a = keep.tile([P, 2, T // 2], F32, name="raw_5a", tag="raw0", align_bytes=64)
         rest = keep.tile([P, 12 * C], U32, name="rest", align_bytes=64)
         raw_end = [raw_5a[:], rest[:, 4 * C : 8 * C].bitcast(F32).rearrange("p (j t) -> p j t", j=2)]
         pairs = keep.tile([P, 2 * PASSES * T * 2], BF16, name="pairs", align_bytes=64)
-        planes = keep.tile([P, 18 * C], U32, name="planes", align_bytes=64)
-        slots_first = raw[4][:, 0, : 2 * C].bitcast(U32)
-        second = raw_5a[:].rearrange("p j t -> p (j t)").bitcast(U32)
-        late, late_second = planes[:, : 2 * C], planes[:, 2 * C : 4 * C]
-        slots_zero = keep.tile([P, 2 * C], U32, name="slots_zero", align_bytes=64)
-        widths = (C, C, 2 * C)
-        x_codes = [keep.tile([P, PASSES * w], U32, name=f"x_codes{g}", align_bytes=64) for g, w in enumerate(widths)]
-        x_scales = {g: keep.tile([P, PASSES * widths[g]], U8, name=f"x_scales{g}", align_bytes=64) for g in (1, 2)}
+        planes = keep.tile([P, 4 * T], U32, name="planes", align_bytes=64)
+        late = work[:, 2 * T :]
+        x_codes = [keep.tile([P, PASSES * 2 * C], U32, name=f"x_codes{g}", align_bytes=64) for g in range(2)]
+        x_scales = [keep.tile([P, PASSES * 2 * C], U8, name=f"x_scales{g}", align_bytes=64) for g in range(2)]
         out_t = [keep.tile([P, T], F32, name=f"out_t{b}") for b in range(NB)]
         h_own = [keep.tile([P, H], BF16, name=f"h{j}", align_bytes=64)[:] for j in range(3)]
         h_act = {0: {0: h_own[0], 1: h_own[1]}, 1: {}, 2: {}, 3: {0: h_own[2]}}
         h_rows = [keep.tile([P, 4 * C], U32, name=f"rows{u}", align_bytes=64) for u in range(E)]
-        h_codes = [keep.tile([P, 2 * C], U32, name=f"h_codes{u}", align_bytes=64) for u in range(E)]
+        h_codes = {u: keep.tile([P, 2 * C], U32, name=f"h_codes{u}", align_bytes=64)[:] for u in (0, 2, 3)}
+        h_codes[1] = x_codes[1][:, : 2 * C]
         h_scales = [keep.tile([P, 2 * C], U8, name=f"h_scales{u}", align_bytes=64) for u in range(E)]
         gated = [keep.tile([P, N], F32, name=f"gated{u}")[:] for u in range(E)]
         ys_rows = [keep.tile([P, N], F32, name=f"ys_rows{u}")[:] for u in range(E)]
@@ -85,6 +88,7 @@ def tile_moe_shr_mlp_gelu_kernel(
         nc.vector.memset(warm[:], 0.0)
         nc.scalar.activation(warm_out[:], warm[:], GELU)
         nc.vector.memset(words(sc1_a), 0)
+        nc.vector.memset(words(sc1_c), 0)
 
         x_rows = xT.rearrange("(s p u j) t -> s u p j t", s=PASSES, p=P, u=2)
         w1_src = w1_words.bitcast(I32)
@@ -93,7 +97,7 @@ def tile_moe_shr_mlp_gelu_kernel(
         w2_sc = w2_scales.bitcast(I32).rearrange("e s (a r) i -> r a (e s) i", r=4)
 
         def load_x(n):
-            nc.sync.dma_start(raw[n][:], x_rows[n // 2, n % 2])
+            nc.sync.dma_start(raw[n], x_rows[n // 2, n % 2])
 
         def load_scales(dst, src, queue):
             for r in range(4):
@@ -109,26 +113,27 @@ def tile_moe_shr_mlp_gelu_kernel(
         nc.sync.dma_start(offsets[:], offs)
         for n in range(1, 5):
             load_x(n)
-        load_scales(sc1_a, w1_sc[:, :, 2 * PASSES :], nc.sync)
+        load_scales(sc1_a, w1_sc[:, :, 3 * PASSES :], nc.sync)
         load_w1_a(0)
         for j in range(2):
             nc.sync.dma_start(raw_end[j], x_rows[2, 1][:, :, j * T // 2 : (j + 1) * T // 2])
         load_w1_a(1)
         for j in range(2):
             nc.sync.dma_start(w1_last[j][:].bitcast(I32), w1_src[3 + j, PASSES - 1])
+        load_scales(sc1_c, w1_sc[:, :, 2 * PASSES : 3 * PASSES], nc.sync)
         load_w1_b(2)
-        load_w1_b(0)
         nc.sync.dma_start(w2_a[:].bitcast(I32), w2_src[:, 2:5])
         nc.sync.dma_start(gate_t[:], gate[0:P, 2 * C :])
+        load_w1_b(0)
         load_w1_b(1)
         with nc.allow_non_contiguous_dma(reason="one gate value a partition"):
             nc.sync.dma_start(gate_col[:], gate[0, : 2 * C].rearrange("(e p) -> p e", p=P))
         nc.sync.dma_start(w2_b[:].bitcast(I32), w2_src[:, 0:2])
 
         def w1_of(e, s):
-            scale = sc1_a[:, (e - 2) * PASSES + s, :] if e >= 2 else sc1_b[:, e * PASSES + s, :]
             if e < 3:
-                return w1_b[e][:, s, :], scale
+                return w1_b[e][:, s, :], sc1_c[:, s, :] if e == 2 else sc1_b[:, e * PASSES + s, :]
+            scale = sc1_a[:, (e - 3) * PASSES + s, :]
             return (w1_a[s][:, e - 3, :] if s < PASSES - 1 else w1_last[e - 3][:]), scale
 
         def w2_of(e):
@@ -142,32 +147,31 @@ def tile_moe_shr_mlp_gelu_kernel(
             copy(dst, src.rearrange("p j t -> p t j"))
 
         def gather(n, lo, hi, dst):
-            window = pairs[:, 2 * block(n) : 2 * (block(n) + T)].bitcast(U32)
+            columns = T if hi - lo < T else WIDE
+            window = pairs[:, 2 * block(n) : 2 * (block(n) + columns)].bitcast(U32)
             nc.vector.tensor_copy(dst, window.indirect(offsets[:, lo // 16 : hi // 16]))
 
-        def interleave(dst, src, copy):
-            two = src.bitcast(F32).rearrange("p (u a) -> p a u", u=2)
-            copy(dst.bitcast(F32).rearrange("p (a u) -> p a u", u=2), two)
-
-        def quantize_x(g, s_lo, s_hi, src):
-            cols = slice(s_lo * widths[g], s_hi * widths[g])
+        def quantize_x(g, lo, hi, src):
             nc.vector.quantize_mx(
-                out=x_codes[g][:, cols].bitcast(FP8X4), scales=x_scales[g][:, cols], in_=src.bitcast(BF16)
+                out=x_codes[g][:, lo:hi].bitcast(FP8X4), scales=x_scales[g][:, lo:hi], in_=src.bitcast(BF16)
             )
 
-        def interleave_early(dst, part, lo, hi, copy):
-            src = part.bitcast(F32).rearrange("p (s u a) -> p s a u", s=2, u=2)[:, :, lo:hi, :]
-            copy(dst.bitcast(F32).rearrange("p (s a u) -> p s a u", s=2, u=2), src)
+        def interleave_early(dst, s_lo, s_hi, lo, hi):
+            src = planes[:].bitcast(F32).rearrange("p (s u a) -> p s a u", s=2, u=2)[:, s_lo:s_hi, lo:hi, :]
+            nc.scalar.copy(dst.bitcast(F32).rearrange("p (s a u) -> p s a u", s=s_hi - s_lo, u=2), src)
 
         acc = {}
 
         def layer1(u, i, s):
             if s == 0:
-                tile = ps_l1.tile([P, H], F32, name="acc")
+                tile = ps_l1.tile([P, H], F32, name=f"acc{u}{i}", tag=ACC_BANK[u, i])
                 acc[u, i] = tile
             w, w_scale = w1_of((ORDER[u], SHARED)[i], s)
-            g = min(u, 2)
-            lo = s * widths[g] + (u - g) * C
+            g = u // 2
+            if g == 0 or s == PASSES - 1:
+                lo = s * 2 * C + ORDER[u] % 2 * C
+            else:
+                lo = ORDER[u] * 2 * C + s * C
             cols = slice(lo, lo + C)
             nc.tensor.matmul_mx(
                 out=acc[u, i][:],
@@ -197,10 +201,15 @@ def tile_moe_shr_mlp_gelu_kernel(
             dst = rows_of(u, lo, hi).bitcast(F32).rearrange("p (i r v) -> p i r v", r=C, v=2)
             copy(dst, src)
 
+        def codes_of(u, lo, hi):
+            if (u, lo) == (0, 0):
+                return x_codes[0][:, 4 * C : 5 * C].bitcast(FP8X4)
+            return h_codes[u][:, lo * C : hi * C].bitcast(FP8X4)
+
         def quantize_h(u, halves):
             lo, hi = halves[0], halves[-1] + 1
             nc.vector.quantize_mx(
-                out=h_codes[u][:, lo * C : hi * C].bitcast(FP8X4),
+                out=codes_of(u, lo, hi),
                 scales=h_scales[u][:, lo * C : hi * C],
                 in_=rows_of(u, lo, hi).bitcast(BF16),
             )
@@ -211,7 +220,7 @@ def tile_moe_shr_mlp_gelu_kernel(
                 out=dst,
                 lhsT=w2_of(e)[:, 2 * P * b : 2 * P * (b + 1)].bitcast(FP4X4),
                 lhsT_scale=sc2[:, e, P * b : P * (b + 1)],
-                rhs=h_codes[u][:, i * C : (i + 1) * C].bitcast(FP8X4),
+                rhs=codes_of(u, i, i + 1),
                 rhs_scale=h_scales[u][:, i * C : (i + 1) * C],
                 start=True,
                 stop=True,
@@ -221,8 +230,10 @@ def tile_moe_shr_mlp_gelu_kernel(
             y = ps_y.tile([P, NB, C], F32, name="y")
             for b in range(NB):
                 layer2(y[:, b, :], u, 0, b)
-            gate_u = gate_t[:, (ORDER[u] - 2) * C : (ORDER[u] - 1) * C].unsqueeze(1).to_broadcast([P, NB, C])
-            nc.vector.tensor_tensor(gated[u].rearrange("p (b c) -> p b c", c=C), y[:], gate_u, MULT)
+            for lo, hi in ((0, 1), (1, NB)) if u == 0 else ((0, NB),):
+                gate_u = gate_t[:, (ORDER[u] - 2) * C : (ORDER[u] - 1) * C].unsqueeze(1).to_broadcast([P, hi - lo, C])
+                dst = gated[u][:, lo * C : hi * C].rearrange("p (b c) -> p b c", c=C)
+                nc.vector.tensor_tensor(dst, y[:, lo:hi, :], gate_u, MULT)
 
         def routed_by_slot(u):
             e = ORDER[u]
@@ -276,68 +287,67 @@ def tile_moe_shr_mlp_gelu_kernel(
         cast(0, raw[0][:, :, :CAST_SPLIT], 0, CAST_SPLIT, vec)
         cast(0, raw[0][:, :, CAST_SPLIT:], CAST_SPLIT, T, act)
         for n in range(1, 5):
-            cast(n, raw[n][:], 0, T, act)
+            cast(n, raw[n], 0, T, act)
         sc2 = keep.tile([P, E + 1, N], U8, name="sc2", tag="raw3", align_bytes=64)
         load_scales(sc2, w2_sc, nc.gpsimd)
-        planes_first, planes_rest = planes[:, 2 * C : 6 * C], planes[:, 6 * C :]
-        x_scales[0] = keep.tile([P, PASSES * C], U8, name="x_scales0", tag="raw2", align_bytes=64)
-        for n in range(4):
-            gather(n, first, T, planes_first[:, (n + 2) % 4 * C : ((n + 2) % 4 + 1) * C])
-            if n == 2:
-                quantize_x(0, 0, 1, slots_zero[:])
-            gather(n, 0, first, planes_rest[:, n * first : (n + 1) * first])
-            if n == 1:
-                interleave(slots_zero[:], planes_first[:, 2 * C :], vec)
-        for i in both:
-            layer1(0, i, 0)
-        interleave(slots_first, planes_first[:, : 2 * C], act)
-        for j in range(2):
-            cast(5, raw_end[j], j * T // 2, (j + 1) * T // 2, act)
-        interleave_early(second, planes_rest, 2 * C, first, act)
-        interleave_early(rest[:, : 8 * C], planes_rest, 0, 2 * C, act)
-        gather_at_step(4, first, T, late)
-        quantize_x(0, 1, 2, slots_first)
-        for i in both:
-            layer1(0, i, 1)
-        sc1_b = keep.tile([P, 2 * PASSES, H], U8, name="sc1_b", tag="raw4", align_bytes=64)
+        for lo in (0, 2 * C):
+            gather(0, lo, lo + 2 * C, planes[:, lo : lo + 2 * C])
+        for n in range(1, 4):
+            gather(n, 0, T, planes[:, n * T : (n + 1) * T])
+        early = [work[:, :T], work[:, T : 2 * T]]
+        for s in range(2):
+            interleave_early(early[s], s, s + 1, 2 * C, T)
+        gather_at_step(4, 2 * C, T, late)
+        quantize_x(0, 0, 2 * C, early[0])
+        gather(4, 0, 2 * C, work[:, : 2 * C])
+        quantize_x(0, 2 * C, 4 * C, early[1])
+        for s in range(2):
+            for u, i in ((0, 0), (0, 1), (1, 1)):
+                layer1(u, i, s)
+        cast(5, raw_end[0], 0, T // 2, act)
+        sc1_b = keep.tile([P, 2 * PASSES, H], U8, name="sc1_b", tag="raw0", align_bytes=64)
         load_scales(sc1_b, w1_sc[:, :, : 2 * PASSES], nc.gpsimd)
-        gather_at_step(4, 2 * C, first, late_second)
-        gather_at_step(5, first, T, late)
-        gather_at_step(5, 2 * C, first, late_second)
-        quantize_x(0, 2, 3, late)
+        cast(5, raw_end[1][:, :, :END_SPLIT], T // 2, T // 2 + END_SPLIT, vec)
+        cast(5, raw_end[1][:, :, END_SPLIT:], T // 2 + END_SPLIT, T, act)
+        by_expert = planes[:].bitcast(F32).rearrange("p (s u e a) -> p e s a u", s=2, u=2, a=C)[:, 0:2]
+        act(rest[:, : 8 * C].bitcast(F32).rearrange("p (e s a u) -> p e s a u", e=2, s=2, u=2), by_expert)
+        gather_at_step(5, first, T, late[:, 2 * C :])
+        gather_at_step(5, 2 * C, first, late[:, : 2 * C])
+        quantize_x(0, 5 * C, 6 * C, late[:, 2 * C :])
         for i in both:
             layer1(0, i, 2)
             activate(0, i)
-        quantize_x(1, 0, 2, second)
-        quantize_x(1, 2, 3, late_second)
-        gather(4, 0, 2 * C, late)
-        gather(5, 0, 2 * C, late_second)
-        quantize_x(2, 0, 2, rest[:, : 8 * C])
-        turn(0, (0,), vec)
-        quantize_h(0, (0,))
-        turn(0, (1,), vec)
-        quantize_h(0, (1,))
+        quantize_x(0, 4 * C, 5 * C, late[:, : 2 * C])
+        layer1(1, 1, 2)
+        activate(1, 1)
+        gather(5, 0, 2 * C, late[:, 2 * C :])
+        two = work[:].bitcast(F32).rearrange("p (u a) -> p a u", u=6)[:, :, 0:6:5]
+        vec(rest[:, 8 * C :].bitcast(F32).rearrange("p (a u) -> p a u", u=2), two)
+        quantize_x(1, 0, 4 * C, rest[:, : 8 * C])
+        quantize_x(1, 4 * C, 6 * C, rest[:, 8 * C :])
 
         def matmuls(u, i):
             for s in range(PASSES):
                 layer1(u, i, s)
 
-        for i in (1, 0):
-            matmuls(1, i)
-            activate(1, i)
-        interleave(rest[:, 8 * C :], planes[:, : 4 * C], act)
-        quantize_x(2, 2, 3, rest[:, 8 * C :])
+        turn(0, (0,), vec)
+        matmuls(1, 0)
+        activate(1, 0)
+        quantize_h(0, (0,))
+        turn(0, (1,), vec)
+        quantize_h(0, (1,))
         routed(0)
         shared(0, [(0, 0), (0, 1)])
         shared_out(0, 0, 0, 0, 1)
         scatter(0, 0)
         turn(1, both, act)
-        quantize_h(1, both)
         for i in (1, 0):
             matmuls(2, i)
-            activate(2, i)
+        quantize_h(1, both)
+        activate(2, 1)
         shared_out(0, 1, 0, 1, 2)
         scatter(0, 1)
+        activate(2, 0)
         routed(1)
         shared(1, [(0, 2), (1, 0), (1, 1), (1, 2)])
         shared_out(1, 0, 0, 2, 3)

@@ -15,7 +15,6 @@ LAST = E - 1
 CAST_SPLIT = 320
 END_SPLIT = 160
 WIDE = 704
-ACC_BANK = {(0, 0): "a", (0, 1): "b", (1, 1): "c", (1, 0): "d", (2, 1): "d", (2, 0): "a", (3, 0): "b", (3, 1): "d"}
 
 F32 = mybir.dt.float32
 BF16 = mybir.dt.bfloat16
@@ -37,7 +36,7 @@ def tile_moe_shr_mlp_gelu_kernel(
     nc = tc.nc
     with ExitStack() as ctx:
         keep = ctx.enter_context(tc.tile_pool(name="keep", bufs=1))
-        ps_l1 = ctx.enter_context(tc.psum_pool(name="ps_l1", bufs=1))
+        ps_l1 = ctx.enter_context(tc.psum_pool(name="ps_l1", bufs=4))
         ps_t = ctx.enter_context(tc.psum_pool(name="ps_t", bufs=2))
         ps_y = ctx.enter_context(tc.psum_pool(name="ps_y", bufs=1))
 
@@ -47,9 +46,10 @@ def tile_moe_shr_mlp_gelu_kernel(
         w1_a = [keep.tile([P, 2, 2 * H], U8, name=f"w1_a{s}", align_bytes=64) for s in range(PASSES - 1)]
         w1_last = [keep.tile([P, 2 * H], U8, name=f"w1_last{j}", align_bytes=64) for j in range(2)]
         w1_b = [keep.tile([P, PASSES, 2 * H], U8, name=f"w1_b{e}", align_bytes=64) for e in range(3)]
-        w2_a = keep.tile([P, 3, 2 * N], U8, name="w2_a", align_bytes=64)
+        w2_a = keep.tile([P, 2, 2 * N], U8, name="w2_a", align_bytes=64)
+        w2_c = keep.tile([P, 2 * N], U8, name="w2_c", align_bytes=64)
         w2_b = keep.tile([P, 2, 2 * N], U8, name="w2_b", align_bytes=64)
-        gate_t = keep.tile([P, 2 * C], F32, name="gate_t")
+        gate_t = [keep.tile([P, C], F32, name=f"gate_t{u}") for u in range(2)]
         ident = keep.tile([P, P], F32, name="ident")
         warm = keep.tile([P, 1], F32, name="warm")
         warm_out = keep.tile([P, 1], F32, name="warm_out")
@@ -118,13 +118,15 @@ def tile_moe_shr_mlp_gelu_kernel(
         for j in range(2):
             nc.sync.dma_start(raw_end[j], x_rows[2, 1][:, :, j * T // 2 : (j + 1) * T // 2])
         load_w1_a(1)
+        load_scales(sc1_c, w1_sc[:, :, 2 * PASSES : 3 * PASSES], nc.sync)
         for j in range(2):
             nc.sync.dma_start(w1_last[j][:].bitcast(I32), w1_src[3 + j, PASSES - 1])
-        load_scales(sc1_c, w1_sc[:, :, 2 * PASSES : 3 * PASSES], nc.sync)
         load_w1_b(2)
-        nc.sync.dma_start(w2_a[:].bitcast(I32), w2_src[:, 2:5])
-        nc.sync.dma_start(gate_t[:], gate[0:P, 2 * C :])
+        nc.sync.dma_start(w2_a[:].bitcast(I32), w2_src[:, 3:5])
         load_w1_b(0)
+        nc.sync.dma_start(gate_t[0][:], gate[0:P, 3 * C :])
+        nc.sync.dma_start(w2_c[:].bitcast(I32), w2_src[:, 2])
+        nc.sync.dma_start(gate_t[1][:], gate[0:P, 2 * C : 3 * C])
         load_w1_b(1)
         with nc.allow_non_contiguous_dma(reason="one gate value a partition"):
             nc.sync.dma_start(gate_col[:], gate[0, : 2 * C].rearrange("(e p) -> p e", p=P))
@@ -137,7 +139,9 @@ def tile_moe_shr_mlp_gelu_kernel(
             return (w1_a[s][:, e - 3, :] if s < PASSES - 1 else w1_last[e - 3][:]), scale
 
         def w2_of(e):
-            return w2_a[:, e - 2, :] if e >= 2 else w2_b[:, e, :]
+            if e == 2:
+                return w2_c[:]
+            return w2_a[:, e - 3, :] if e > 2 else w2_b[:, e, :]
 
         def block(n):
             return (2 * PASSES - 1 - n) * T
@@ -164,7 +168,7 @@ def tile_moe_shr_mlp_gelu_kernel(
 
         def layer1(u, i, s):
             if s == 0:
-                tile = ps_l1.tile([P, H], F32, name=f"acc{u}{i}", tag=ACC_BANK[u, i])
+                tile = ps_l1.tile([P, H], F32, name="acc")
                 acc[u, i] = tile
             w, w_scale = w1_of((ORDER[u], SHARED)[i], s)
             g = u // 2
@@ -202,8 +206,6 @@ def tile_moe_shr_mlp_gelu_kernel(
             copy(dst, src)
 
         def codes_of(u, lo, hi):
-            if (u, lo) == (0, 0):
-                return x_codes[0][:, 4 * C : 5 * C].bitcast(FP8X4)
             return h_codes[u][:, lo * C : hi * C].bitcast(FP8X4)
 
         def quantize_h(u, halves):
@@ -231,7 +233,7 @@ def tile_moe_shr_mlp_gelu_kernel(
             for b in range(NB):
                 layer2(y[:, b, :], u, 0, b)
             for lo, hi in ((0, 1), (1, NB)) if u == 0 else ((0, NB),):
-                gate_u = gate_t[:, (ORDER[u] - 2) * C : (ORDER[u] - 1) * C].unsqueeze(1).to_broadcast([P, hi - lo, C])
+                gate_u = gate_t[u][:].unsqueeze(1).to_broadcast([P, hi - lo, C])
                 dst = gated[u][:, lo * C : hi * C].rearrange("p (b c) -> p b c", c=C)
                 nc.vector.tensor_tensor(dst, y[:, lo:hi, :], gate_u, MULT)
 
@@ -330,12 +332,11 @@ def tile_moe_shr_mlp_gelu_kernel(
             for s in range(PASSES):
                 layer1(u, i, s)
 
-        turn(0, (0,), vec)
+        for i in both:
+            turn(0, (i,), vec)
+            quantize_h(0, (i,))
         matmuls(1, 0)
         activate(1, 0)
-        quantize_h(0, (0,))
-        turn(0, (1,), vec)
-        quantize_h(0, (1,))
         routed(0)
         shared(0, [(0, 0), (0, 1)])
         shared_out(0, 0, 0, 0, 1)

@@ -290,8 +290,6 @@ def tile_moe_shr_mlp_gelu_kernel(
         cast(0, raw[0][:, :, CAST_SPLIT:], CAST_SPLIT, T, act)
         for n in range(1, 5):
             cast(n, raw[n], 0, T, act)
-        sc2 = keep.tile([P, E + 1, N], U8, name="sc2", tag="raw3", align_bytes=64)
-        load_scales(sc2, w2_sc, nc.gpsimd)
         for lo in (0, 2 * C):
             gather(0, lo, lo + 2 * C, planes[:, lo : lo + 2 * C])
         for n in range(1, 4):
@@ -313,6 +311,8 @@ def tile_moe_shr_mlp_gelu_kernel(
         cast(5, raw_end[1][:, :, END_SPLIT:], T // 2 + END_SPLIT, T, act)
         by_expert = planes[:].bitcast(F32).rearrange("p (s u e a) -> p e s a u", s=2, u=2, a=C)[:, 0:2]
         act(rest[:, : 8 * C].bitcast(F32).rearrange("p (e s a u) -> p e s a u", e=2, s=2, u=2), by_expert)
+        sc2 = keep.tile([P, E + 1, N], U8, name="sc2", tag="planes", align_bytes=64)
+        load_scales(sc2, w2_sc, nc.scalar)
         gather_at_step(5, first, T, late[:, 2 * C :])
         gather_at_step(5, 2 * C, first, late[:, : 2 * C])
         quantize_x(0, 5 * C, 6 * C, late[:, 2 * C :])

@@ -12,6 +12,8 @@ PASSES = K // 512
 NB = N // P
 ORDER = (3, 2, 0, 1)
 LAST = E - 1
+ROUTED, COMMON = 0, 1
+BOTH = (ROUTED, COMMON)
 CAST_SPLIT = 320
 END_SPLIT = 160
 WIDE = 704
@@ -44,7 +46,7 @@ def tile_moe_shr_mlp_gelu_kernel(
         sc1_a = keep.tile([P, 2 * PASSES, H], U8, name="sc1_a", align_bytes=64)
         sc1_c = keep.tile([P, PASSES, H], U8, name="sc1_c", align_bytes=64)
         w1_a = [keep.tile([P, 2, 2 * H], U8, name=f"w1_a{s}", align_bytes=64) for s in range(PASSES - 1)]
-        w1_last = [keep.tile([P, 2 * H], U8, name=f"w1_last{j}", align_bytes=64) for j in range(2)]
+        w1_last = [keep.tile([P, 2 * H], U8, name=f"w1_last{mat}", align_bytes=64) for mat in BOTH]
         w1_b = [keep.tile([P, PASSES, 2 * H], U8, name=f"w1_b{e}", align_bytes=64) for e in range(3)]
         w2_a = keep.tile([P, 2, 2 * N], U8, name="w2_a", align_bytes=64)
         w2_c = keep.tile([P, 2 * N], U8, name="w2_c", align_bytes=64)
@@ -53,20 +55,19 @@ def tile_moe_shr_mlp_gelu_kernel(
         ident = keep.tile([P, P], F32, name="ident")
         warm = keep.tile([P, 1], F32, name="warm")
         warm_out = keep.tile([P, 1], F32, name="warm_out")
-        raw = [keep.tile([P, 2, T], F32, name=f"raw{n}", align_bytes=64)[:] for n in range(2 * PASSES - 2)]
+        raw = [keep.tile([P, 2, T], F32, name=f"raw{chunk}", align_bytes=64)[:] for chunk in range(4)]
         work = keep.tile([P, 3 * T], U32, name="work", align_bytes=64)
-        raw.append(work[:, : 2 * T].bitcast(F32).rearrange("p (j t) -> p j t", j=2))
+        raw.append(work[:, : 2 * T].bitcast(F32).rearrange("p (member t) -> p member t", member=2))
         raw_5a = keep.tile([P, 2, T // 2], F32, name="raw_5a", tag="raw0", align_bytes=64)
         rest = keep.tile([P, 12 * C], U32, name="rest", align_bytes=64)
-        raw_end = [raw_5a[:], rest[:, 4 * C : 8 * C].bitcast(F32).rearrange("p (j t) -> p j t", j=2)]
+        raw_end = [raw_5a[:], rest[:, 4 * C : 8 * C].bitcast(F32).rearrange("p (member t) -> p member t", member=2)]
         pairs = keep.tile([P, 2 * PASSES * T * 2], BF16, name="pairs", align_bytes=64)
         planes = keep.tile([P, 4 * T], U32, name="planes", align_bytes=64)
         late = work[:, 2 * T :]
         x_codes = [keep.tile([P, PASSES * 2 * C], U32, name=f"x_codes{g}", align_bytes=64) for g in range(2)]
         x_scales = [keep.tile([P, PASSES * 2 * C], U8, name=f"x_scales{g}", align_bytes=64) for g in range(2)]
         out_t = [keep.tile([P, T], F32, name=f"out_t{b}") for b in range(NB)]
-        h_own = [keep.tile([P, H], BF16, name=f"h{j}", align_bytes=64)[:] for j in range(3)]
-        h_act = {0: {0: h_own[0], 1: h_own[1]}, 1: {}, 2: {}, 3: {0: h_own[2]}}
+        h_own = [keep.tile([P, H], BF16, name=f"h{own}", align_bytes=64)[:] for own in range(3)]
         h_rows = [keep.tile([P, 4 * C], U32, name=f"rows{u}", align_bytes=64) for u in range(E)]
         h_codes = {u: keep.tile([P, 2 * C], U32, name=f"h_codes{u}", align_bytes=64)[:] for u in (0, 2, 3)}
         h_codes[1] = x_codes[1][:, : 2 * C]
@@ -75,14 +76,19 @@ def tile_moe_shr_mlp_gelu_kernel(
         ys_rows = [keep.tile([P, N], F32, name=f"ys_rows{u}")[:] for u in range(E)]
         by_slot = [keep.tile([P, N], F32, name=f"by_slot{e}") for e in range(2)]
         gate_col = keep.tile([P, 2], F32, name="gate_col")
-        h_act[1][1] = ys_rows[0][:, C:].bitcast(BF16)
-        h_act[1][0] = ys_rows[1][:, C:].bitcast(BF16)
-        h_act[2][1] = h_act[1][0]
-        h_act[2][0] = gated[2][:, C:].bitcast(BF16)
-        h_act[3][1] = h_act[2][0]
+        h_act = {
+            (0, ROUTED): h_own[0],
+            (0, COMMON): h_own[1],
+            (1, COMMON): ys_rows[0][:, C:].bitcast(BF16),
+            (1, ROUTED): ys_rows[1][:, C:].bitcast(BF16),
+            (2, ROUTED): gated[2][:, C:].bitcast(BF16),
+            (3, ROUTED): h_own[2],
+        }
+        h_act[2, COMMON] = h_act[1, ROUTED]
+        h_act[3, COMMON] = h_act[2, ROUTED]
 
         def words(tile):
-            return tile[:].rearrange("p a i -> p (a i)").bitcast(I32)
+            return tile[:].rearrange("p s i -> p (s i)").bitcast(I32)
 
         make_identity(nc, ident[:])
         nc.vector.memset(warm[:], 0.0)
@@ -90,41 +96,41 @@ def tile_moe_shr_mlp_gelu_kernel(
         nc.vector.memset(words(sc1_a), 0)
         nc.vector.memset(words(sc1_c), 0)
 
-        x_rows = xT.rearrange("(s p u j) t -> s u p j t", s=PASSES, p=P, u=2)
+        x_rows = xT.rearrange("(s p z member) t -> s z p member t", s=PASSES, p=P, z=2)
         w1_src = w1_words.bitcast(I32)
-        w2_src = w2_words.bitcast(I32).rearrange("e a p b -> p (e a) b")
-        w1_sc = w1_scales.bitcast(I32).rearrange("e s (a r) i -> r a (e s) i", r=4)
-        w2_sc = w2_scales.bitcast(I32).rearrange("e s (a r) i -> r a (e s) i", r=4)
+        w2_src = w2_words.bitcast(I32).rearrange("e s p w -> p (e s) w")
+        w1_sc = w1_scales.bitcast(I32).rearrange("e s (quad r) w -> r quad (e s) w", r=4)
+        w2_sc = w2_scales.bitcast(I32).rearrange("e s (quad r) w -> r quad (e s) w", r=4)
 
-        def load_x(n):
-            nc.sync.dma_start(raw[n], x_rows[n // 2, n % 2])
+        def load_x(chunk):
+            nc.sync.dma_start(raw[chunk], x_rows[chunk // 2, chunk % 2])
 
         def load_scales(dst, src, queue):
             for r in range(4):
                 queue.dma_start(dst[r:P:32].bitcast(I32), src[r])
 
         def load_w1_a(s):
-            nc.sync.dma_start(w1_a[s][:].bitcast(I32), w1_src[3:5, s].rearrange("e p b -> p e b"))
+            nc.sync.dma_start(w1_a[s][:].bitcast(I32), w1_src[3:5, s].rearrange("e p w -> p e w"))
 
         def load_w1_b(e):
-            nc.sync.dma_start(w1_b[e][:].bitcast(I32), w1_src[e].rearrange("s p b -> p s b"))
+            nc.sync.dma_start(w1_b[e][:].bitcast(I32), w1_src[e].rearrange("s p w -> p s w"))
 
         load_x(0)
         nc.sync.dma_start(offsets[:], offs)
-        for n in range(1, 5):
-            load_x(n)
+        for chunk in range(1, 5):
+            load_x(chunk)
         load_scales(sc1_a, w1_sc[:, :, 3 * PASSES :], nc.sync)
         load_w1_a(0)
-        for j in range(2):
-            nc.sync.dma_start(raw_end[j], x_rows[2, 1][:, :, j * T // 2 : (j + 1) * T // 2])
+        for half in range(2):
+            nc.sync.dma_start(raw_end[half], x_rows[2, 1][:, :, half * T // 2 : (half + 1) * T // 2])
         load_w1_a(1)
         load_scales(sc1_c, w1_sc[:, :, 2 * PASSES : 3 * PASSES], nc.sync)
-        for j in range(2):
-            nc.sync.dma_start(w1_last[j][:].bitcast(I32), w1_src[3 + j, PASSES - 1])
+        for mat in BOTH:
+            nc.sync.dma_start(w1_last[mat][:].bitcast(I32), w1_src[3 + mat, PASSES - 1])
         load_w1_b(2)
         nc.sync.dma_start(w2_a[:].bitcast(I32), w2_src[:, 3:5])
-        load_w1_b(0)
         nc.sync.dma_start(gate_t[0][:], gate[0:P, 3 * C :])
+        load_w1_b(0)
         nc.sync.dma_start(w2_c[:].bitcast(I32), w2_src[:, 2])
         nc.sync.dma_start(gate_t[1][:], gate[0:P, 2 * C : 3 * C])
         load_w1_b(1)
@@ -143,34 +149,37 @@ def tile_moe_shr_mlp_gelu_kernel(
                 return w2_c[:]
             return w2_a[:, e - 3, :] if e > 2 else w2_b[:, e, :]
 
-        def block(n):
-            return (2 * PASSES - 1 - n) * T
+        def first_pair(chunk):
+            return (2 * PASSES - 1 - chunk) * T
 
-        def cast(n, src, lo, hi, copy):
-            dst = pairs[:, 2 * (block(n) + lo) : 2 * (block(n) + hi)].rearrange("p (t j) -> p t j", j=2)
-            copy(dst, src.rearrange("p j t -> p t j"))
+        def cast(chunk, src, lo, hi, copy):
+            dst = pairs[:, 2 * (first_pair(chunk) + lo) : 2 * (first_pair(chunk) + hi)]
+            copy(dst.rearrange("p (t member) -> p t member", member=2), src.rearrange("p member t -> p t member"))
 
-        def gather(n, lo, hi, dst):
+        def gather(chunk, lo, hi, dst):
             columns = T if hi - lo < T else WIDE
-            window = pairs[:, 2 * block(n) : 2 * (block(n) + columns)].bitcast(U32)
+            window = pairs[:, 2 * first_pair(chunk) : 2 * (first_pair(chunk) + columns)].bitcast(U32)
             nc.vector.tensor_copy(dst, window.indirect(offsets[:, lo // 16 : hi // 16]))
+
+        def gather_laid_out(chunk, lo, hi, dst):
+            gather(chunk, lo, hi, dst.rearrange("p (slot z) -> p slot z", z=2)[:, :, chunk % 2])
 
         def quantize_x(g, lo, hi, src):
             nc.vector.quantize_mx(
                 out=x_codes[g][:, lo:hi].bitcast(FP8X4), scales=x_scales[g][:, lo:hi], in_=src.bitcast(BF16)
             )
 
-        def interleave_early(dst, s_lo, s_hi, lo, hi):
-            src = planes[:].bitcast(F32).rearrange("p (s u a) -> p s a u", s=2, u=2)[:, s_lo:s_hi, lo:hi, :]
-            nc.scalar.copy(dst.bitcast(F32).rearrange("p (s a u) -> p s a u", s=s_hi - s_lo, u=2), src)
+        def lay_out_early(dst, s):
+            src = planes[:].bitcast(F32).rearrange("p (s z slot) -> p s slot z", s=2, z=2)[:, s : s + 1, 2 * C : T, :]
+            nc.scalar.copy(dst.bitcast(F32).rearrange("p (s slot z) -> p s slot z", s=1, z=2), src)
 
         acc = {}
 
-        def layer1(u, i, s):
+        def layer1(u, mat, s):
             if s == 0:
                 tile = ps_l1.tile([P, H], F32, name="acc")
-                acc[u, i] = tile
-            w, w_scale = w1_of((ORDER[u], SHARED)[i], s)
+                acc[u, mat] = tile
+            w, w_scale = w1_of((ORDER[u], SHARED)[mat], s)
             g = u // 2
             if g == 0 or s == PASSES - 1:
                 lo = s * 2 * C + ORDER[u] % 2 * C
@@ -178,7 +187,7 @@ def tile_moe_shr_mlp_gelu_kernel(
                 lo = ORDER[u] * 2 * C + s * C
             cols = slice(lo, lo + C)
             nc.tensor.matmul_mx(
-                out=acc[u, i][:],
+                out=acc[u, mat][:],
                 lhsT=x_codes[g][:, cols].bitcast(FP8X4),
                 lhsT_scale=x_scales[g][:, cols],
                 rhs=w.bitcast(FP4X4),
@@ -187,43 +196,45 @@ def tile_moe_shr_mlp_gelu_kernel(
                 stop=(s == PASSES - 1),
             )
 
-        def activate(u, i):
-            src = acc[u, i][:].rearrange("p (m v d) -> p v m d", v=2, d=2)
-            nc.scalar.activation(h_act[u][i].rearrange("p (v m d) -> p v m d", v=2, d=2), src, GELU)
+        def layer1_whole(u, mat):
+            for s in range(PASSES):
+                layer1(u, mat, s)
+
+        def activate(u, mat):
+            src = acc[u, mat][:].rearrange("p (m v member) -> p v m member", v=2, member=2)
+            dst = h_act[u, mat].rearrange("p (v m member) -> p v m member", v=2, member=2)
+            nc.scalar.activation(dst, src, GELU)
 
         def rows_of(u, lo, hi):
             return h_rows[u][:, 2 * C * lo : 2 * C * hi]
 
-        def turn(u, halves, copy):
+        def turn(u, matrices, copy):
             bank = ps_t.tile([P, 4, C], F32, name="bank")
-            for i in halves:
-                h_words = h_act[u][i].bitcast(F32)
+            for mat in matrices:
+                h_words = h_act[u, mat].bitcast(F32)
                 for v in range(2):
-                    nc.tensor.transpose(bank[:, 2 * i + v, :], h_words[:, v * P : (v + 1) * P], ident[:])
-            lo, hi = halves[0], halves[-1] + 1
-            src = bank[:, 2 * lo : 2 * hi, :].rearrange("p (i v) r -> p i r v", v=2)
-            dst = rows_of(u, lo, hi).bitcast(F32).rearrange("p (i r v) -> p i r v", r=C, v=2)
+                    nc.tensor.transpose(bank[:, 2 * mat + v, :], h_words[:, v * P : (v + 1) * P], ident[:])
+            lo, hi = matrices[0], matrices[-1] + 1
+            src = bank[:, 2 * lo : 2 * hi, :].rearrange("p (mat v) slot -> p mat slot v", v=2)
+            dst = rows_of(u, lo, hi).bitcast(F32).rearrange("p (mat slot v) -> p mat slot v", slot=C, v=2)
             copy(dst, src)
 
-        def codes_of(u, lo, hi):
-            return h_codes[u][:, lo * C : hi * C].bitcast(FP8X4)
-
-        def quantize_h(u, halves):
-            lo, hi = halves[0], halves[-1] + 1
+        def quantize_h(u, matrices):
+            lo, hi = matrices[0], matrices[-1] + 1
             nc.vector.quantize_mx(
-                out=codes_of(u, lo, hi),
+                out=h_codes[u][:, lo * C : hi * C].bitcast(FP8X4),
                 scales=h_scales[u][:, lo * C : hi * C],
                 in_=rows_of(u, lo, hi).bitcast(BF16),
             )
 
-        def layer2(dst, u, i, b):
-            e = (ORDER[u], SHARED)[i]
+        def layer2(dst, u, mat, b):
+            e = (ORDER[u], SHARED)[mat]
             nc.tensor.matmul_mx(
                 out=dst,
                 lhsT=w2_of(e)[:, 2 * P * b : 2 * P * (b + 1)].bitcast(FP4X4),
                 lhsT_scale=sc2[:, e, P * b : P * (b + 1)],
-                rhs=codes_of(u, i, i + 1),
-                rhs_scale=h_scales[u][:, i * C : (i + 1) * C],
+                rhs=h_codes[u][:, mat * C : (mat + 1) * C].bitcast(FP8X4),
+                rhs_scale=h_scales[u][:, mat * C : (mat + 1) * C],
                 start=True,
                 stop=True,
             )
@@ -231,10 +242,10 @@ def tile_moe_shr_mlp_gelu_kernel(
         def routed(u):
             y = ps_y.tile([P, NB, C], F32, name="y")
             for b in range(NB):
-                layer2(y[:, b, :], u, 0, b)
+                layer2(y[:, b, :], u, ROUTED, b)
             for lo, hi in ((0, 1), (1, NB)) if u == 0 else ((0, NB),):
                 gate_u = gate_t[u][:].unsqueeze(1).to_broadcast([P, hi - lo, C])
-                dst = gated[u][:, lo * C : hi * C].rearrange("p (b c) -> p b c", c=C)
+                dst = gated[u][:, lo * C : hi * C].rearrange("p (b slot) -> p b slot", slot=C)
                 nc.vector.tensor_tensor(dst, y[:, lo:hi, :], gate_u, MULT)
 
         def routed_by_slot(u):
@@ -259,119 +270,108 @@ def tile_moe_shr_mlp_gelu_kernel(
             for lo, hi in ((0, P), (P, N)) if u == LAST else ((0, N),):
                 nc.scalar.copy(gated[u][:, lo:hi], y[:, lo:hi])
 
-        ys_bank = {}
-
-        def shared(u, blocks):
+        def shared(blocks):
             ys = ps_y.tile([P, 4 * C], F32, name="ys")
-            ys_bank[u] = ys
-            for j, (v, b) in enumerate(blocks):
-                layer2(ys[:, j * C : (j + 1) * C], v, 1, b)
+            for place, (u, b) in enumerate(blocks):
+                layer2(ys[:, place * C : (place + 1) * C], u, COMMON, b)
+            return ys
 
-        def ys_of(u, b):
-            return ys_rows[u][:, b * C : (b + 1) * C]
-
-        def shared_out(u, at, v, lo, hi):
-            nc.scalar.copy(ys_rows[v][:, lo * C : hi * C], ys_bank[u][:, at * C : (at + hi - lo) * C])
+        def shared_out(ys, place, u, lo, hi):
+            nc.scalar.copy(ys_rows[u][:, lo * C : hi * C], ys[:, place * C : (place + hi - lo) * C])
 
         def scatter(u, b):
             where = offsets[:, ORDER[u] * C // 16 : (ORDER[u] + 1) * C // 16]
-            nc.vector.tensor_tensor(out_t[b][:].indirect(where), gated[u][:, b * C : (b + 1) * C], ys_of(u, b), ADD)
+            cols = slice(b * C, (b + 1) * C)
+            nc.vector.tensor_tensor(out_t[b][:].indirect(where), gated[u][:, cols], ys_rows[u][:, cols], ADD)
             if u == LAST:
                 nc.sync.dma_start(out[b * P : (b + 1) * P, :], out_t[b][:])
 
         vec, act = nc.vector.tensor_copy, nc.scalar.copy
-        both = (0, 1)
-        first = 3 * C
-
-        def gather_at_step(n, lo, hi, dst):
-            gather(n, lo, hi, dst.rearrange("p (a u) -> p a u", u=2)[:, :, n % 2])
 
         cast(0, raw[0][:, :, :CAST_SPLIT], 0, CAST_SPLIT, vec)
         cast(0, raw[0][:, :, CAST_SPLIT:], CAST_SPLIT, T, act)
-        for n in range(1, 5):
-            cast(n, raw[n], 0, T, act)
+        for chunk in range(1, 5):
+            cast(chunk, raw[chunk], 0, T, act)
         for lo in (0, 2 * C):
             gather(0, lo, lo + 2 * C, planes[:, lo : lo + 2 * C])
-        for n in range(1, 4):
-            gather(n, 0, T, planes[:, n * T : (n + 1) * T])
+        for chunk in range(1, 4):
+            gather(chunk, 0, T, planes[:, chunk * T : (chunk + 1) * T])
         early = [work[:, :T], work[:, T : 2 * T]]
         for s in range(2):
-            interleave_early(early[s], s, s + 1, 2 * C, T)
-        gather_at_step(4, 2 * C, T, late)
+            lay_out_early(early[s], s)
+        gather_laid_out(4, 2 * C, T, late)
         quantize_x(0, 0, 2 * C, early[0])
         gather(4, 0, 2 * C, work[:, : 2 * C])
         quantize_x(0, 2 * C, 4 * C, early[1])
         for s in range(2):
-            for u, i in ((0, 0), (0, 1), (1, 1)):
-                layer1(u, i, s)
+            for u, mat in ((0, ROUTED), (0, COMMON), (1, COMMON)):
+                layer1(u, mat, s)
+
         cast(5, raw_end[0], 0, T // 2, act)
         sc1_b = keep.tile([P, 2 * PASSES, H], U8, name="sc1_b", tag="raw0", align_bytes=64)
         load_scales(sc1_b, w1_sc[:, :, : 2 * PASSES], nc.gpsimd)
         cast(5, raw_end[1][:, :, :END_SPLIT], T // 2, T // 2 + END_SPLIT, vec)
         cast(5, raw_end[1][:, :, END_SPLIT:], T // 2 + END_SPLIT, T, act)
-        by_expert = planes[:].bitcast(F32).rearrange("p (s u e a) -> p e s a u", s=2, u=2, a=C)[:, 0:2]
-        act(rest[:, : 8 * C].bitcast(F32).rearrange("p (e s a u) -> p e s a u", e=2, s=2, u=2), by_expert)
+        by_expert = planes[:].bitcast(F32).rearrange("p (s z e slot) -> p e s slot z", s=2, z=2, slot=C)[:, 0:2]
+        act(rest[:, : 8 * C].bitcast(F32).rearrange("p (e s slot z) -> p e s slot z", e=2, s=2, z=2), by_expert)
         sc2 = keep.tile([P, E + 1, N], U8, name="sc2", tag="planes", align_bytes=64)
         load_scales(sc2, w2_sc, nc.scalar)
-        gather_at_step(5, first, T, late[:, 2 * C :])
-        gather_at_step(5, 2 * C, first, late[:, : 2 * C])
+        gather_laid_out(5, 3 * C, T, late[:, 2 * C :])
+        gather_laid_out(5, 2 * C, 3 * C, late[:, : 2 * C])
         quantize_x(0, 5 * C, 6 * C, late[:, 2 * C :])
-        for i in both:
-            layer1(0, i, 2)
-            activate(0, i)
+        for mat in BOTH:
+            layer1(0, mat, 2)
+            activate(0, mat)
         quantize_x(0, 4 * C, 5 * C, late[:, : 2 * C])
-        layer1(1, 1, 2)
-        activate(1, 1)
+        layer1(1, COMMON, 2)
+        activate(1, COMMON)
         gather(5, 0, 2 * C, late[:, 2 * C :])
-        two = work[:].bitcast(F32).rearrange("p (u a) -> p a u", u=6)[:, :, 0:6:5]
-        vec(rest[:, 8 * C :].bitcast(F32).rearrange("p (a u) -> p a u", u=2), two)
+        last_planes = work[:].bitcast(F32).rearrange("p (sixth slot) -> p slot sixth", sixth=6)[:, :, 0:6:5]
+        vec(rest[:, 8 * C :].bitcast(F32).rearrange("p (slot z) -> p slot z", z=2), last_planes)
         quantize_x(1, 0, 4 * C, rest[:, : 8 * C])
         quantize_x(1, 4 * C, 6 * C, rest[:, 8 * C :])
 
-        def matmuls(u, i):
-            for s in range(PASSES):
-                layer1(u, i, s)
-
-        for i in both:
-            turn(0, (i,), vec)
-            quantize_h(0, (i,))
-        matmuls(1, 0)
-        activate(1, 0)
+        for mat in BOTH:
+            turn(0, (mat,), vec)
+            quantize_h(0, (mat,))
+        layer1_whole(1, ROUTED)
+        activate(1, ROUTED)
         routed(0)
-        shared(0, [(0, 0), (0, 1)])
-        shared_out(0, 0, 0, 0, 1)
+        ys = shared([(0, 0), (0, 1)])
+        shared_out(ys, 0, 0, 0, 1)
         scatter(0, 0)
-        turn(1, both, act)
-        for i in (1, 0):
-            matmuls(2, i)
-        quantize_h(1, both)
-        activate(2, 1)
-        shared_out(0, 1, 0, 1, 2)
+
+        turn(1, BOTH, act)
+        for mat in (COMMON, ROUTED):
+            layer1_whole(2, mat)
+        quantize_h(1, BOTH)
+        activate(2, COMMON)
+        shared_out(ys, 1, 0, 1, 2)
         scatter(0, 1)
-        activate(2, 0)
+        activate(2, ROUTED)
         routed(1)
-        shared(1, [(0, 2), (1, 0), (1, 1), (1, 2)])
-        shared_out(1, 0, 0, 2, 3)
+        ys = shared([(0, 2)] + [(1, b) for b in range(NB)])
+        shared_out(ys, 0, 0, 2, 3)
         scatter(0, 2)
-        turn(2, both, act)
-        quantize_h(2, both)
-        shared_out(1, 1, 1, 0, NB)
+
+        turn(2, BOTH, act)
+        quantize_h(2, BOTH)
+        shared_out(ys, 1, 1, 0, NB)
         for b in range(NB):
             scatter(1, b)
-        for i in both:
-            matmuls(3, i)
-            activate(3, i)
+        for mat in BOTH:
+            layer1_whole(3, mat)
+            activate(3, mat)
         routed_by_slot(2)
-        shared(2, [(2, b) for b in range(NB)])
-        shared_out(2, 0, 2, 0, NB)
-        turn(3, both, act)
-        quantize_h(3, both)
+        shared_out(shared([(2, b) for b in range(NB)]), 0, 2, 0, NB)
+
+        turn(3, BOTH, act)
+        quantize_h(3, BOTH)
         turn_back(2)
         for b in range(NB):
             scatter(2, b)
         routed_by_slot(3)
-        shared(3, [(3, b) for b in range(NB)])
-        shared_out(3, 0, 3, 0, NB)
+        shared_out(shared([(3, b) for b in range(NB)]), 0, 3, 0, NB)
         turn_back(3)
         for b in range(NB):
             scatter(3, b)

@@ -11,9 +11,6 @@ SHARED = E
 PASSES = K // 512
 NB = N // P
 ORDER = (3, 2, 0, 1)
-LAST = E - 1
-ROUTED, COMMON = 0, 1
-BOTH = (ROUTED, COMMON)
 CAST_SPLIT = 320
 END_SPLIT = 160
 WIDE = 704
@@ -38,63 +35,54 @@ def tile_moe_shr_mlp_gelu_kernel(
     nc = tc.nc
     with ExitStack() as ctx:
         keep = ctx.enter_context(tc.tile_pool(name="keep", bufs=1))
-        ps_l1 = ctx.enter_context(tc.psum_pool(name="ps_l1", bufs=4))
-        ps_t = ctx.enter_context(tc.psum_pool(name="ps_t", bufs=2))
-        ps_y = ctx.enter_context(tc.psum_pool(name="ps_y", bufs=1))
+        reuse = ctx.enter_context(tc.tile_pool(name="reuse", bufs=1))
+        psum = ctx.enter_context(tc.psum_pool(name="psum", bufs=1))
 
         offsets = keep.tile([P, E * C // 16], U16, name="offsets")
-        sc1_a = keep.tile([P, 2 * PASSES, H], U8, name="sc1_a", align_bytes=64)
-        sc1_c = keep.tile([P, PASSES, H], U8, name="sc1_c", align_bytes=64)
-        w1_a = [keep.tile([P, 2, 2 * H], U8, name=f"w1_a{s}", align_bytes=64) for s in range(PASSES - 1)]
-        w1_last = [keep.tile([P, 2 * H], U8, name=f"w1_last{mat}", align_bytes=64) for mat in BOTH]
-        w1_b = [keep.tile([P, PASSES, 2 * H], U8, name=f"w1_b{e}", align_bytes=64) for e in range(3)]
-        w2_a = keep.tile([P, 2, 2 * N], U8, name="w2_a", align_bytes=64)
-        w2_c = keep.tile([P, 2 * N], U8, name="w2_c", align_bytes=64)
-        w2_b = keep.tile([P, 2, 2 * N], U8, name="w2_b", align_bytes=64)
-        gate_t = [keep.tile([P, C], F32, name=f"gate_t{u}") for u in range(2)]
+        sc1_early = keep.tile([P, 2 * PASSES, H], U8, name="sc1_early", align_bytes=64)
+        w1_shared = [keep.tile([P, n, 2 * H], U8, name=f"w1_shared{n}", align_bytes=64) for n in (1, 2)]
+        own_at = {0: 25600, 1: 12288, 2: 22528, 3: 28672}
+        w1_own = [
+            reuse.tile([P, PASSES, 2 * H], U8, name=f"w1_own{e}", offset=own_at[e], align_bytes=64) for e in range(E)
+        ]
+        w2_early = keep.tile([P, 3, 2 * N], U8, name="w2_early", align_bytes=64)
+        w2_late = keep.tile([P, 2, 2 * N], U8, name="w2_late", align_bytes=64)
+        gate_t = [keep.tile([P, 2 * C], F32, name=f"gate_t{g}") for g in range(2)]
         ident = keep.tile([P, P], F32, name="ident")
         warm = keep.tile([P, 1], F32, name="warm")
         warm_out = keep.tile([P, 1], F32, name="warm_out")
-        raw = [keep.tile([P, 2, T], F32, name=f"raw{chunk}", align_bytes=64)[:] for chunk in range(4)]
-        work = keep.tile([P, 3 * T], U32, name="work", align_bytes=64)
-        raw.append(work[:, : 2 * T].bitcast(F32).rearrange("p (member t) -> p member t", member=2))
-        raw_5a = keep.tile([P, 2, T // 2], F32, name="raw_5a", tag="raw0", align_bytes=64)
-        rest = keep.tile([P, 12 * C], U32, name="rest", align_bytes=64)
-        raw_end = [raw_5a[:], rest[:, 4 * C : 8 * C].bitcast(F32).rearrange("p (member t) -> p member t", member=2)]
-        pairs = keep.tile([P, 2 * PASSES * T * 2], BF16, name="pairs", align_bytes=64)
+        raw = {c: keep.tile([P, 2, T], F32, name=f"raw{c}", align_bytes=64) for c in (0, 4)}
+        raw[1] = reuse.tile([P, 2, T], F32, name="raw1", offset=0, align_bytes=64)
+        raw[2] = reuse.tile([P, 2, T], F32, name="raw2", offset=40960, align_bytes=64)
+        raw[3] = reuse.tile([P, 2, T], F32, name="raw3", offset=4096, align_bytes=64)
+        raw_end = [
+            reuse.tile([P, 2, T // 2], F32, name="raw_5a", offset=36864 - 2048, align_bytes=64),
+            keep.tile([P, 2, T // 2], F32, name="raw_5b", align_bytes=64),
+        ]
+        pairs = keep.tile([P, 6 * T * 2], BF16, name="pairs", align_bytes=64)
         planes = keep.tile([P, 4 * T], U32, name="planes", align_bytes=64)
-        late = work[:, 2 * T :]
+        late = keep.tile([P, 4 * C], U32, name="late", align_bytes=64)
+        laid2 = keep.tile([P, T], U32, name="laid2", align_bytes=64)
         x_codes = [keep.tile([P, PASSES * 2 * C], U32, name=f"x_codes{g}", align_bytes=64) for g in range(2)]
         x_scales = [keep.tile([P, PASSES * 2 * C], U8, name=f"x_scales{g}", align_bytes=64) for g in range(2)]
-        out_t = [keep.tile([P, T], F32, name=f"out_t{b}") for b in range(NB)]
-        h_own = [keep.tile([P, H], BF16, name=f"h{own}", align_bytes=64)[:] for own in range(3)]
-        h_rows = [keep.tile([P, 4 * C], U32, name=f"rows{u}", align_bytes=64) for u in range(E)]
-        h_codes = {u: keep.tile([P, 2 * C], U32, name=f"h_codes{u}", align_bytes=64)[:] for u in (0, 2, 3)}
-        h_codes[1] = x_codes[1][:, : 2 * C]
-        h_scales = [keep.tile([P, 2 * C], U8, name=f"h_scales{u}", align_bytes=64) for u in range(E)]
-        gated = [keep.tile([P, N], F32, name=f"gated{u}")[:] for u in range(E)]
-        ys_rows = [keep.tile([P, N], F32, name=f"ys_rows{u}")[:] for u in range(E)]
-        by_slot = [keep.tile([P, N], F32, name=f"by_slot{e}") for e in range(2)]
-        gate_col = keep.tile([P, 2], F32, name="gate_col")
-        h_act = {
-            (0, ROUTED): h_own[0],
-            (0, COMMON): h_own[1],
-            (1, COMMON): ys_rows[0][:, C:].bitcast(BF16),
-            (1, ROUTED): ys_rows[1][:, C:].bitcast(BF16),
-            (2, ROUTED): gated[2][:, C:].bitcast(BF16),
-            (3, ROUTED): h_own[2],
-        }
-        h_act[2, COMMON] = h_act[1, ROUTED]
-        h_act[3, COMMON] = h_act[2, ROUTED]
-
-        def words(tile):
-            return tile[:].rearrange("p s i -> p (s i)").bitcast(I32)
+        out_t = {0: keep.tile([P, T], F32, name="out_t0")}
+        h_act = {}
+        act_at = {("s", 1): own_at[ORDER[1]], ("s", 3): 45056}
+        units = {"r0": [("r", 0)], "s0": [("s", 0)], "b1": [("r", 1), ("s", 1)],
+                 "b2": [("r", 2), ("s", 2)], "b3": [("r", 3), ("s", 3)]}
+        rows_at = {"r0": 32768, "s0": 33792, "b1": 51200, "b2": 18432, "b3": 47104}
+        h_rows = {}
+        h_codes = {n: keep.tile([P, C * len(ms)], U32, name=f"codes{n}", align_bytes=64) for n, ms in units.items()}
+        h_codes = {n: tile[:] for n, tile in h_codes.items()}
+        h_scales = {n: keep.tile([P, C * len(ms)], U8, name=f"hsc{n}", align_bytes=64) for n, ms in units.items()}
+        gated = [keep.tile([P, N], F32, name=f"gated{u}") for u in range(E)]
+        total = [keep.tile([P, 2 * C], F32, name=f"total{u}") for u in range(E)]
+        ys_rows = [keep.tile([P, 2 * C], F32, name=f"ys_rows{u}") for u in range(E)]
 
         make_identity(nc, ident[:])
         nc.vector.memset(warm[:], 0.0)
         nc.scalar.activation(warm_out[:], warm[:], GELU)
-        nc.vector.memset(words(sc1_a), 0)
-        nc.vector.memset(words(sc1_c), 0)
+        nc.vector.memset(sc1_early[:].rearrange("p s i -> p (s i)").bitcast(I32), 0)
 
         x_rows = xT.rearrange("(s p z member) t -> s z p member t", s=PASSES, p=P, z=2)
         w1_src = w1_words.bitcast(I32)
@@ -103,275 +91,283 @@ def tile_moe_shr_mlp_gelu_kernel(
         w2_sc = w2_scales.bitcast(I32).rearrange("e s (quad r) w -> r quad (e s) w", r=4)
 
         def load_x(chunk):
-            nc.sync.dma_start(raw[chunk], x_rows[chunk // 2, chunk % 2])
+            nc.sync.dma_start(raw[chunk][:], x_rows[chunk // 2, chunk % 2])
 
         def load_scales(dst, src, queue):
             for r in range(4):
                 queue.dma_start(dst[r:P:32].bitcast(I32), src[r])
 
-        def load_w1_a(s):
-            nc.sync.dma_start(w1_a[s][:].bitcast(I32), w1_src[3:5, s].rearrange("e p w -> p e w"))
+        def load_shared(part, lo, hi):
+            nc.sync.dma_start(w1_shared[part][:].bitcast(I32), w1_src[SHARED, lo:hi].rearrange("s p w -> p s w"))
 
-        def load_w1_b(e):
-            nc.sync.dma_start(w1_b[e][:].bitcast(I32), w1_src[e].rearrange("s p w -> p s w"))
+        def load_own(e):
+            nc.sync.dma_start(w1_own[e][:].bitcast(I32), w1_src[e].rearrange("s p w -> p s w"))
 
-        load_x(0)
-        nc.sync.dma_start(offsets[:], offs)
-        for chunk in range(1, 5):
-            load_x(chunk)
-        load_scales(sc1_a, w1_sc[:, :, 3 * PASSES :], nc.sync)
-        load_w1_a(0)
-        for half in range(2):
-            nc.sync.dma_start(raw_end[half], x_rows[2, 1][:, :, half * T // 2 : (half + 1) * T // 2])
-        load_w1_a(1)
-        load_scales(sc1_c, w1_sc[:, :, 2 * PASSES : 3 * PASSES], nc.sync)
-        for mat in BOTH:
-            nc.sync.dma_start(w1_last[mat][:].bitcast(I32), w1_src[3 + mat, PASSES - 1])
-        load_w1_b(2)
-        nc.sync.dma_start(w2_a[:].bitcast(I32), w2_src[:, 3:5])
-        nc.sync.dma_start(gate_t[0][:], gate[0:P, 3 * C :])
-        load_w1_b(0)
-        nc.sync.dma_start(w2_c[:].bitcast(I32), w2_src[:, 2])
-        nc.sync.dma_start(gate_t[1][:], gate[0:P, 2 * C : 3 * C])
-        load_w1_b(1)
-        with nc.allow_non_contiguous_dma(reason="one gate value a partition"):
-            nc.sync.dma_start(gate_col[:], gate[0, : 2 * C].rearrange("(e p) -> p e", p=P))
-        nc.sync.dma_start(w2_b[:].bitcast(I32), w2_src[:, 0:2])
+        late_tiles = {}
 
         def w1_of(e, s):
+            words = w1_shared[min(s, 1)][:, max(s - 1, 0), :] if e == SHARED else w1_own[e][:, s, :]
             if e < 3:
-                return w1_b[e][:, s, :], sc1_c[:, s, :] if e == 2 else sc1_b[:, e * PASSES + s, :]
-            scale = sc1_a[:, (e - 3) * PASSES + s, :]
-            return (w1_a[s][:, e - 3, :] if s < PASSES - 1 else w1_last[e - 3][:]), scale
+                return words, late_tiles["sc1"][:, e * PASSES + s, :]
+            return words, sc1_early[:, (e - 3) * PASSES + s, :]
 
         def w2_of(e):
-            if e == 2:
-                return w2_c[:]
-            return w2_a[:, e - 3, :] if e > 2 else w2_b[:, e, :]
+            return w2_late[:, e, :] if e < 2 else w2_early[:, e - 2, :]
 
         def first_pair(chunk):
             return (2 * PASSES - 1 - chunk) * T
 
+        def pairs_of(chunk, lo, hi):
+            return pairs[:, 2 * (first_pair(chunk) + lo) : 2 * (first_pair(chunk) + hi)]
+
         def cast(chunk, src, lo, hi, copy):
-            dst = pairs[:, 2 * (first_pair(chunk) + lo) : 2 * (first_pair(chunk) + hi)]
+            dst = pairs_of(chunk, lo, hi)
             copy(dst.rearrange("p (t member) -> p t member", member=2), src.rearrange("p member t -> p t member"))
 
         def gather(chunk, lo, hi, dst):
             columns = T if hi - lo < T else WIDE
-            window = pairs[:, 2 * first_pair(chunk) : 2 * (first_pair(chunk) + columns)].bitcast(U32)
+            window = pairs_of(chunk, 0, columns).bitcast(U32)
             nc.vector.tensor_copy(dst, window.indirect(offsets[:, lo // 16 : hi // 16]))
 
         def gather_laid_out(chunk, lo, hi, dst):
             gather(chunk, lo, hi, dst.rearrange("p (slot z) -> p slot z", z=2)[:, :, chunk % 2])
+
+        def lay_out(dst, src, first, second, copy):
+            halves = src.bitcast(F32).rearrange("p (n slot) -> p slot n", slot=2 * C)
+            both = halves[:, :, first : second + 1 : second - first]
+            copy(dst.bitcast(F32).rearrange("p (slot z) -> p slot z", z=2), both)
 
         def quantize_x(g, lo, hi, src):
             nc.vector.quantize_mx(
                 out=x_codes[g][:, lo:hi].bitcast(FP8X4), scales=x_scales[g][:, lo:hi], in_=src.bitcast(BF16)
             )
 
-        def lay_out_early(dst, s):
-            src = planes[:].bitcast(F32).rearrange("p (s z slot) -> p s slot z", s=2, z=2)[:, s : s + 1, 2 * C : T, :]
-            nc.scalar.copy(dst.bitcast(F32).rearrange("p (s slot z) -> p s slot z", s=1, z=2), src)
+        def bank(n, name):
+            return psum.tile([P, 4 * C], F32, name=name, tag=f"bank{n}")
 
         acc = {}
 
-        def layer1(u, mat, s):
+        def layer1(m, s, n=None):
+            kind, u = m
             if s == 0:
-                tile = ps_l1.tile([P, H], F32, name="acc")
-                acc[u, mat] = tile
-            w, w_scale = w1_of((ORDER[u], SHARED)[mat], s)
-            g = u // 2
-            if g == 0 or s == PASSES - 1:
-                lo = s * 2 * C + ORDER[u] % 2 * C
-            else:
-                lo = ORDER[u] * 2 * C + s * C
+                acc[m] = bank(n, f"acc{kind}{u}")
+            w, w_scale = w1_of(ORDER[u] if kind == "r" else SHARED, s)
+            lo = (2 * s + ORDER[u] % 2) * C
             cols = slice(lo, lo + C)
             nc.tensor.matmul_mx(
-                out=acc[u, mat][:],
-                lhsT=x_codes[g][:, cols].bitcast(FP8X4),
-                lhsT_scale=x_scales[g][:, cols],
+                out=acc[m][:],
+                lhsT=x_codes[u // 2][:, cols].bitcast(FP8X4),
+                lhsT_scale=x_scales[u // 2][:, cols],
                 rhs=w.bitcast(FP4X4),
                 rhs_scale=w_scale,
                 start=(s == 0),
                 stop=(s == PASSES - 1),
             )
 
-        def layer1_whole(u, mat):
+        def layer1_whole(m, n):
             for s in range(PASSES):
-                layer1(u, mat, s)
+                layer1(m, s, n)
 
-        def activate(u, mat):
-            src = acc[u, mat][:].rearrange("p (m v member) -> p v m member", v=2, member=2)
-            dst = h_act[u, mat].rearrange("p (v m member) -> p v m member", v=2, member=2)
+        def activate(m):
+            kind, u = m
+            if m in act_at:
+                h_act[m] = reuse.tile([P, H], BF16, name=f"h_act{kind}{u}", offset=act_at[m], align_bytes=64)
+            else:
+                h_act[m] = keep.tile([P, H], BF16, name=f"h_act{kind}{u}", align_bytes=64)
+            src = acc[m][:].rearrange("p (m v member) -> p v m member", v=2, member=2)
+            dst = h_act[m][:].rearrange("p (v m member) -> p v m member", v=2, member=2)
             nc.scalar.activation(dst, src, GELU)
 
-        def rows_of(u, lo, hi):
-            return h_rows[u][:, 2 * C * lo : 2 * C * hi]
-
-        def turn(u, matrices, copy):
-            bank = ps_t.tile([P, 4, C], F32, name="bank")
-            for mat in matrices:
-                h_words = h_act[u, mat].bitcast(F32)
+        def turn(unit, n, copy):
+            ms = units[unit]
+            turned = bank(n, f"turned{unit}")
+            for place, m in enumerate(ms):
+                h_words = h_act[m][:].bitcast(F32)
                 for v in range(2):
-                    nc.tensor.transpose(bank[:, 2 * mat + v, :], h_words[:, v * P : (v + 1) * P], ident[:])
-            lo, hi = matrices[0], matrices[-1] + 1
-            src = bank[:, 2 * lo : 2 * hi, :].rearrange("p (mat v) slot -> p mat slot v", v=2)
-            dst = rows_of(u, lo, hi).bitcast(F32).rearrange("p (mat slot v) -> p mat slot v", slot=C, v=2)
+                    cols = slice((2 * place + v) * C, (2 * place + v + 1) * C)
+                    nc.tensor.transpose(turned[:, cols], h_words[:, v * P : (v + 1) * P], ident[:])
+            h_rows[unit] = reuse.tile([P, 2 * C * len(ms)], U32, name=f"rows{unit}", offset=rows_at[unit], align_bytes=64)
+            src = turned[:, : 2 * C * len(ms)].rearrange("p (mat v slot) -> p mat slot v", v=2, slot=C)
+            dst = h_rows[unit][:].bitcast(F32).rearrange("p (mat slot v) -> p mat slot v", slot=C, v=2)
             copy(dst, src)
 
-        def quantize_h(u, matrices):
-            lo, hi = matrices[0], matrices[-1] + 1
+        def quantize_h(unit):
             nc.vector.quantize_mx(
-                out=h_codes[u][:, lo * C : hi * C].bitcast(FP8X4),
-                scales=h_scales[u][:, lo * C : hi * C],
-                in_=rows_of(u, lo, hi).bitcast(BF16),
+                out=h_codes[unit].bitcast(FP8X4), scales=h_scales[unit][:], in_=h_rows[unit][:].bitcast(BF16)
             )
 
-        def layer2(dst, u, mat, b):
-            e = (ORDER[u], SHARED)[mat]
-            nc.tensor.matmul_mx(
-                out=dst,
-                lhsT=w2_of(e)[:, 2 * P * b : 2 * P * (b + 1)].bitcast(FP4X4),
-                lhsT_scale=sc2[:, e, P * b : P * (b + 1)],
-                rhs=h_codes[u][:, mat * C : (mat + 1) * C].bitcast(FP8X4),
-                rhs_scale=h_scales[u][:, mat * C : (mat + 1) * C],
-                start=True,
-                stop=True,
-            )
-
-        def routed(u):
-            y = ps_y.tile([P, NB, C], F32, name="y")
-            for b in range(NB):
-                layer2(y[:, b, :], u, ROUTED, b)
-            for lo, hi in ((0, 1), (1, NB)) if u == 0 else ((0, NB),):
-                gate_u = gate_t[u][:].unsqueeze(1).to_broadcast([P, hi - lo, C])
-                dst = gated[u][:, lo * C : hi * C].rearrange("p (b slot) -> p b slot", slot=C)
-                nc.vector.tensor_tensor(dst, y[:, lo:hi, :], gate_u, MULT)
-
-        def routed_by_slot(u):
-            e = ORDER[u]
-            y = ps_y.tile([P, N], F32, name="y")
-            for lo, hi in ((0, 2 * P), (2 * P, N)):
+        def layer2(m, blocks, dst):
+            kind, u = m
+            e = ORDER[u] if kind == "r" else SHARED
+            unit, place = (f"{kind}{u}", 0) if u < 1 else (f"b{u}", ("r", "s").index(kind))
+            cols = slice(place * C, (place + 1) * C)
+            for at, b in enumerate(blocks):
                 nc.tensor.matmul_mx(
-                    out=y[:, lo:hi],
-                    lhsT=h_codes[u][:, :C].bitcast(FP8X4),
-                    lhsT_scale=h_scales[u][:, :C],
-                    rhs=w2_of(e)[:, 2 * lo : 2 * hi].bitcast(FP4X4),
-                    rhs_scale=sc2[:, e, lo:hi],
+                    out=dst[:, at * C : (at + 1) * C],
+                    lhsT=w2_of(e)[:, 2 * P * b : 2 * P * (b + 1)].bitcast(FP4X4),
+                    lhsT_scale=late_tiles["sc2"][:, e, P * b : P * (b + 1)],
+                    rhs=h_codes[unit][:, cols].bitcast(FP8X4),
+                    rhs_scale=h_scales[unit][:, cols],
                     start=True,
                     stop=True,
                 )
-            nc.scalar.activation(by_slot[e][:], y[:], COPY, scale=gate_col[:, e : e + 1])
 
-        def turn_back(u):
-            y = ps_y.tile([P, N], F32, name="y")
-            for b in range(NB):
-                nc.tensor.transpose(y[:, b * P : (b + 1) * P], by_slot[ORDER[u]][:, b * P : (b + 1) * P], ident[:])
-            for lo, hi in ((0, P), (P, N)) if u == LAST else ((0, N),):
-                nc.scalar.copy(gated[u][:, lo:hi], y[:, lo:hi])
+        def blocks_of(ap, blocks):
+            return ap.rearrange("p (b slot) -> p b slot", slot=C)[:, blocks, :]
 
-        def shared(blocks):
-            ys = ps_y.tile([P, 4 * C], F32, name="ys")
-            for place, (u, b) in enumerate(blocks):
-                layer2(ys[:, place * C : (place + 1) * C], u, COMMON, b)
-            return ys
+        def times_gate(u, y, blocks, dst):
+            place = ORDER[u] % 2
+            src = blocks_of(y[:, :N], blocks)
+            gate_u = gate_t[u // 2][:, place * C : (place + 1) * C].unsqueeze(1).to_broadcast(list(src.shape))
+            nc.vector.tensor_tensor(dst, src, gate_u, MULT)
 
-        def shared_out(ys, place, u, lo, hi):
-            nc.scalar.copy(ys_rows[u][:, lo * C : hi * C], ys[:, place * C : (place + hi - lo) * C])
+        def where(u, lo=0, hi=C):
+            return offsets[:, (ORDER[u] * C + lo) // 16 : (ORDER[u] * C + hi) // 16]
 
-        def scatter(u, b):
-            where = offsets[:, ORDER[u] * C // 16 : (ORDER[u] + 1) * C // 16]
-            cols = slice(b * C, (b + 1) * C)
-            nc.vector.tensor_tensor(out_t[b][:].indirect(where), gated[u][:, cols], ys_rows[u][:, cols], ADD)
-            if u == LAST:
-                nc.sync.dma_start(out[b * P : (b + 1) * P, :], out_t[b][:])
+        def scatter_sum(u, b, gated_block):
+            nc.vector.tensor_tensor(out_t[b][:].indirect(where(u)), gated_block, ys_rows[u][:, b * C : (b + 1) * C], ADD)
+
+        def scatter_vector(u, b, src, lo=0, hi=C):
+            nc.vector.tensor_copy(out_t[b][:].indirect(where(u, lo, hi)), src[:, lo:hi])
+
+        def scatter_scalar(u, b, src, lo=0, hi=C):
+            nc.scalar.activation(out_t[b][:].indirect(where(u, lo, hi)), src[:, lo:hi], COPY)
+
+        def store(b):
+            nc.sync.dma_start(out[b * P : (b + 1) * P, :], out_t[b][:])
 
         vec, act = nc.vector.tensor_copy, nc.scalar.copy
 
+        load_x(0)
+        nc.sync.dma_start(offsets[:], offs)
+        for chunk in range(1, 4):
+            load_x(chunk)
         cast(0, raw[0][:, :, :CAST_SPLIT], 0, CAST_SPLIT, vec)
         cast(0, raw[0][:, :, CAST_SPLIT:], CAST_SPLIT, T, act)
-        for chunk in range(1, 5):
-            cast(chunk, raw[chunk], 0, T, act)
-        for lo in (0, 2 * C):
-            gather(0, lo, lo + 2 * C, planes[:, lo : lo + 2 * C])
+        late_tiles["sc2"] = keep.tile([P, E + 1, N], U8, name="sc2", tag="raw0", align_bytes=64)
+        load_scales(late_tiles["sc2"], w2_sc, nc.sync)
+        load_x(4)
+        load_scales(sc1_early, w1_sc[:, :, 3 * PASSES :], nc.sync)
+        load_shared(0, 0, 1)
+        for half in range(2):
+            nc.sync.dma_start(raw_end[half][:], x_rows[2, 1][:, :, half * T // 2 : (half + 1) * T // 2])
+        load_own(3)
+        load_shared(1, 1, 3)
+        load_own(2)
+        load_own(0)
+        nc.sync.dma_start(w2_early[:].bitcast(I32), w2_src[:, 2:5])
+        nc.sync.dma_start(gate_t[0][:], gate[0:P, 2 * C :])
+        load_own(1)
+        nc.sync.dma_start(gate_t[1][:], gate[0:P, : 2 * C])
+        nc.sync.dma_start(w2_late[:].bitcast(I32), w2_src[:, 0:2])
+        for chunk in range(1, 4):
+            cast(chunk, raw[chunk][:], 0, T, act)
+        gather(0, 2 * C, T, planes[:, 2 * C : T])
+        gather(0, 0, 2 * C, planes[:, :2 * C])
         for chunk in range(1, 4):
             gather(chunk, 0, T, planes[:, chunk * T : (chunk + 1) * T])
-        early = [work[:, :T], work[:, T : 2 * T]]
-        for s in range(2):
-            lay_out_early(early[s], s)
-        gather_laid_out(4, 2 * C, T, late)
-        quantize_x(0, 0, 2 * C, early[0])
-        gather(4, 0, 2 * C, work[:, : 2 * C])
-        quantize_x(0, 2 * C, 4 * C, early[1])
-        for s in range(2):
-            for u, mat in ((0, ROUTED), (0, COMMON), (1, COMMON)):
-                layer1(u, mat, s)
+        late_tiles["sc1"] = reuse.tile([P, 3 * PASSES, H], U8, name="sc1_late", offset=0, align_bytes=64)
+        load_scales(late_tiles["sc1"], w1_sc[:, :, : 3 * PASSES], nc.gpsimd)
+        laid0 = reuse.tile([P, T], U32, name="laid0", offset=6144, align_bytes=64)
+        lay_out(laid0[:], planes[:], 1, 3, act)
+        quantize_x(0, 0, 2 * C, laid0[:])
+        cast(4, raw[4][:], 0, T, act)
+        laid1 = keep.tile([P, T], U32, name="laid1", tag="raw4", align_bytes=64)
+        lay_out(laid1[:], planes[:], 5, 7, act)
+        gather_laid_out(4, 2 * C, T, late[:])
+        for u in range(2):
+            layer1(("s", u), 0, u)
+        quantize_x(0, 2 * C, 4 * C, laid1[:])
 
-        cast(5, raw_end[0], 0, T // 2, act)
-        sc1_b = keep.tile([P, 2 * PASSES, H], U8, name="sc1_b", tag="raw0", align_bytes=64)
-        load_scales(sc1_b, w1_sc[:, :, : 2 * PASSES], nc.gpsimd)
-        cast(5, raw_end[1][:, :, :END_SPLIT], T // 2, T // 2 + END_SPLIT, vec)
-        cast(5, raw_end[1][:, :, END_SPLIT:], T // 2 + END_SPLIT, T, act)
-        by_expert = planes[:].bitcast(F32).rearrange("p (s z e slot) -> p e s slot z", s=2, z=2, slot=C)[:, 0:2]
-        act(rest[:, : 8 * C].bitcast(F32).rearrange("p (e s slot z) -> p e s slot z", e=2, s=2, z=2), by_expert)
-        sc2 = keep.tile([P, E + 1, N], U8, name="sc2", tag="planes", align_bytes=64)
-        load_scales(sc2, w2_sc, nc.scalar)
+        cast(5, raw_end[0][:], 0, T // 2, act)
+        cast(5, raw_end[1][:], T // 2, T, vec)
+        laid_late = reuse.tile([P, 2 * T], U32, name="laid_late", offset=36864 - 128, align_bytes=64)
+        late_src = planes[:].bitcast(F32).rearrange("p (s z slot) -> p s slot z", s=2, z=2)[:, :, : 2 * C, :]
+        act(laid_late[:].bitcast(F32).rearrange("p (s slot z) -> p s slot z", s=2, z=2), late_src)
         gather_laid_out(5, 3 * C, T, late[:, 2 * C :])
         gather_laid_out(5, 2 * C, 3 * C, late[:, : 2 * C])
         quantize_x(0, 5 * C, 6 * C, late[:, 2 * C :])
-        for mat in BOTH:
-            layer1(0, mat, 2)
-            activate(0, mat)
         quantize_x(0, 4 * C, 5 * C, late[:, : 2 * C])
-        layer1(1, COMMON, 2)
-        activate(1, COMMON)
         gather(5, 0, 2 * C, late[:, 2 * C :])
-        last_planes = work[:].bitcast(F32).rearrange("p (sixth slot) -> p slot sixth", sixth=6)[:, :, 0:6:5]
-        vec(rest[:, 8 * C :].bitcast(F32).rearrange("p (slot z) -> p slot z", z=2), last_planes)
-        quantize_x(1, 0, 4 * C, rest[:, : 8 * C])
-        quantize_x(1, 4 * C, 6 * C, rest[:, 8 * C :])
+        gather(4, 0, 2 * C, late[:, : 2 * C])
+        quantize_x(1, 0, 4 * C, laid_late[:])
+        lay_out(laid2[:], late[:], 0, 1, vec)
+        quantize_x(1, 4 * C, 6 * C, laid2[:])
 
-        for mat in BOTH:
-            turn(0, (mat,), vec)
-            quantize_h(0, (mat,))
-        layer1_whole(1, ROUTED)
-        activate(1, ROUTED)
-        routed(0)
-        ys = shared([(0, 0), (0, 1)])
-        shared_out(ys, 0, 0, 0, 1)
-        scatter(0, 0)
-
-        turn(1, BOTH, act)
-        for mat in (COMMON, ROUTED):
-            layer1_whole(2, mat)
-        quantize_h(1, BOTH)
-        activate(2, COMMON)
-        shared_out(ys, 1, 0, 1, 2)
-        scatter(0, 1)
-        activate(2, ROUTED)
-        routed(1)
-        ys = shared([(0, 2)] + [(1, b) for b in range(NB)])
-        shared_out(ys, 0, 0, 2, 3)
-        scatter(0, 2)
-
-        turn(2, BOTH, act)
-        quantize_h(2, BOTH)
-        shared_out(ys, 1, 1, 0, NB)
-        for b in range(NB):
-            scatter(1, b)
-        for mat in BOTH:
-            layer1_whole(3, mat)
-            activate(3, mat)
-        routed_by_slot(2)
-        shared_out(shared([(2, b) for b in range(NB)]), 0, 2, 0, NB)
-
-        turn(3, BOTH, act)
-        quantize_h(3, BOTH)
-        turn_back(2)
-        for b in range(NB):
-            scatter(2, b)
-        routed_by_slot(3)
-        shared_out(shared([(3, b) for b in range(NB)]), 0, 3, 0, NB)
-        turn_back(3)
-        for b in range(NB):
-            scatter(3, b)
+        r = [("r", u) for u in range(E)]
+        s_ = [("s", u) for u in range(E)]
+        layer1_whole(r[0], 2)
+        activate(r[0])
+        for s in (1, 2):
+            layer1(s_[0], s)
+        activate(s_[0])
+        turn("r0", 3, act)
+        turn("s0", 4, act)
+        layer1_whole(r[1], 5)
+        for s in (1, 2):
+            layer1(s_[1], s)
+        quantize_h("r0")
+        quantize_h("s0")
+        activate(r[1])
+        activate(s_[1])
+        layer1_whole(r[2], 6)
+        y, ys = bank(2, "y0"), bank(0, "ys0")
+        layer2(r[0], (0, 1, 2), y)
+        layer2(s_[0], (0, 1), ys)
+        layer2(s_[0], (2,), y[:, N:])
+        times_gate(0, y, slice(0, 3), blocks_of(gated[0][:], slice(0, 3)))
+        act(ys_rows[0][:], ys[:, : 2 * C])
+        nc.vector.tensor_tensor(total[0][:, :C], y[:, N:], gated[0][:, 2 * C :], ADD)
+        activate(r[2])
+        turn("b1", 5, act)
+        layer1_whole(s_[2], 3)
+        scatter_sum(0, 0, gated[0][:, :C])
+        quantize_h("b1")
+        activate(s_[2])
+        layer1_whole(r[3], 2)
+        activate(r[3])
+        y, ys = bank(7, "y1"), bank(1, "ys1")
+        layer2(r[1], (0, 1, 2), y)
+        layer2(s_[1], (0, 1, 2), ys)
+        out_t[1] = reuse.tile([P, T], F32, name="out_t1", offset=rows_at["b1"] - 1024, align_bytes=64)
+        scatter_sum(0, 1, gated[0][:, C : 2 * C])
+        out_t[2] = reuse.tile([P, T], F32, name="out_t2", offset=rows_at["b1"] + 1024, align_bytes=64)
+        scatter_scalar(0, 2, total[0])
+        times_gate(1, y, slice(0, 3), blocks_of(gated[1][:], slice(0, 3)))
+        turn("b2", 4, act)
+        layer1_whole(s_[3], 3)
+        activate(s_[3])
+        quantize_h("b2")
+        total[1] = reuse.tile([P, 2 * C], F32, name="total1", offset=rows_at["b2"], align_bytes=64)
+        nc.vector.tensor_tensor(total[1][:], ys[:, : 2 * C], gated[1][:, : 2 * C], ADD)
+        ys1 = ys
+        y, ys = bank(5, "y2"), bank(6, "ys2")
+        layer2(r[2], (0, 1, 2), y)
+        layer2(s_[2], (0, 1, 2), ys)
+        scatter_vector(1, 0, total[1][:, :C])
+        turn("b3", 4, act)
+        scatter_scalar(1, 1, total[1][:, C : 2 * C])
+        times_gate(2, y, slice(0, 3), blocks_of(gated[2][:], slice(0, 3)))
+        last1 = reuse.tile([P, C], F32, name="last1", offset=act_at["s", 3], align_bytes=64)
+        nc.vector.tensor_tensor(last1[:], ys1[:, 2 * C : N], gated[1][:, 2 * C :], ADD)
+        quantize_h("b3")
+        scatter_scalar(1, 2, last1)
+        total[2] = reuse.tile([P, N], F32, name="total2", offset=rows_at["b3"], align_bytes=64)
+        nc.vector.tensor_tensor(total[2][:], ys[:, :N], gated[2][:], ADD)
+        y, ys, ys_first = bank(2, "y3"), bank(7, "ys3"), bank(0, "ys3a")
+        layer2(r[3], (0, 1, 2), y)
+        layer2(s_[3], (1, 2), ys)
+        layer2(s_[3], (0,), ys_first)
+        scatter_scalar(2, 1, total[2][:, C : 2 * C])
+        scatter_vector(2, 0, total[2][:, :C])
+        times_gate(3, y, slice(0, 3), blocks_of(gated[3][:], slice(0, 3)))
+        act(ys_rows[3][:, :C], ys_first[:, :C])
+        scatter_scalar(2, 2, total[2][:, 2 * C :])
+        nc.vector.tensor_tensor(total[3][:], ys[:, : 2 * C], gated[3][:, C:], ADD)
+        scatter_sum(3, 0, gated[3][:, :C])
+        store(0)
+        scatter_scalar(3, 1, total[3], 0, C // 2)
+        scatter_scalar(3, 2, total[3][:, C:])
+        store(2)
+        nc.vector.tensor_copy(out_t[1][:].indirect(where(3, C // 2, C)), total[3][:, C // 2 : C])
+        store(1)

@@ -39,7 +39,7 @@ def tile_moe_shr_mlp_gelu_kernel(
         psum = ctx.enter_context(tc.psum_pool(name="psum", bufs=1))
 
         offsets = keep.tile([P, E * C // 16], U16, name="offsets")
-        sc1_early = keep.tile([P, 2 * PASSES, H], U8, name="sc1_early", align_bytes=64)
+        sc1_early = keep.tile([P, 3 * PASSES, H], U8, name="sc1_early", align_bytes=64)
         w1_shared = [keep.tile([P, n, 2 * H], U8, name=f"w1_shared{n}", align_bytes=64) for n in (1, 2)]
         own_at = {0: 25600, 1: 12288, 2: 22528, 3: 28672}
         w1_own = [
@@ -51,7 +51,8 @@ def tile_moe_shr_mlp_gelu_kernel(
         ident = keep.tile([P, P], F32, name="ident")
         warm = keep.tile([P, 1], F32, name="warm")
         warm_out = keep.tile([P, 1], F32, name="warm_out")
-        raw = {c: keep.tile([P, 2, T], F32, name=f"raw{c}", align_bytes=64) for c in (0, 4)}
+        raw = {c: keep.tile([P, 2, T], F32, name=f"raw{c}", align_bytes=64) for c in (0,)}
+        raw[4] = reuse.tile([P, 2, T], F32, name="raw4", offset=57344, align_bytes=64)
         raw[1] = reuse.tile([P, 2, T], F32, name="raw1", offset=0, align_bytes=64)
         raw[2] = reuse.tile([P, 2, T], F32, name="raw2", offset=40960, align_bytes=64)
         raw[3] = reuse.tile([P, 2, T], F32, name="raw3", offset=4096, align_bytes=64)
@@ -107,9 +108,9 @@ def tile_moe_shr_mlp_gelu_kernel(
 
         def w1_of(e, s):
             words = w1_shared[min(s, 1)][:, max(s - 1, 0), :] if e == SHARED else w1_own[e][:, s, :]
-            if e < 3:
+            if e < 2:
                 return words, late_tiles["sc1"][:, e * PASSES + s, :]
-            return words, sc1_early[:, (e - 3) * PASSES + s, :]
+            return words, sc1_early[:, (e - 2) * PASSES + s, :]
 
         def w2_of(e):
             return w2_late[:, e, :] if e < 2 else w2_early[:, e - 2, :]
@@ -247,16 +248,16 @@ def tile_moe_shr_mlp_gelu_kernel(
         late_tiles["sc2"] = keep.tile([P, E + 1, N], U8, name="sc2", tag="raw0", align_bytes=64)
         load_scales(late_tiles["sc2"], w2_sc, nc.sync)
         load_x(4)
-        load_scales(sc1_early, w1_sc[:, :, 3 * PASSES :], nc.sync)
+        load_scales(sc1_early, w1_sc[:, :, 2 * PASSES :], nc.sync)
         load_shared(0, 0, 1)
         for half in range(2):
             nc.sync.dma_start(raw_end[half][:], x_rows[2, 1][:, :, half * T // 2 : (half + 1) * T // 2])
         load_own(3)
         load_shared(1, 1, 3)
         load_own(2)
-        load_own(0)
         nc.sync.dma_start(w2_early[:].bitcast(I32), w2_src[:, 2:5])
         nc.sync.dma_start(gate_t[0][:], gate[0:P, 2 * C :])
+        load_own(0)
         load_own(1)
         nc.sync.dma_start(gate_t[1][:], gate[0:P, : 2 * C])
         nc.sync.dma_start(w2_late[:].bitcast(I32), w2_src[:, 0:2])
@@ -266,13 +267,13 @@ def tile_moe_shr_mlp_gelu_kernel(
         gather(0, 0, 2 * C, planes[:, :2 * C])
         for chunk in range(1, 4):
             gather(chunk, 0, T, planes[:, chunk * T : (chunk + 1) * T])
-        late_tiles["sc1"] = reuse.tile([P, 3 * PASSES, H], U8, name="sc1_late", offset=0, align_bytes=64)
-        load_scales(late_tiles["sc1"], w1_sc[:, :, : 3 * PASSES], nc.gpsimd)
         laid0 = reuse.tile([P, T], U32, name="laid0", offset=6144, align_bytes=64)
         lay_out(laid0[:], planes[:], 1, 3, act)
         quantize_x(0, 0, 2 * C, laid0[:])
         cast(4, raw[4][:], 0, T, act)
-        laid1 = keep.tile([P, T], U32, name="laid1", tag="raw4", align_bytes=64)
+        late_tiles["sc1"] = reuse.tile([P, 2 * PASSES, H], U8, name="sc1_late", offset=57344, align_bytes=64)
+        load_scales(late_tiles["sc1"], w1_sc[:, :, : 2 * PASSES], nc.gpsimd)
+        laid1 = reuse.tile([P, T], U32, name="laid1", offset=57344 + 3072, align_bytes=64)
         lay_out(laid1[:], planes[:], 5, 7, act)
         gather_laid_out(4, 2 * C, T, late[:])
         for u in range(2):
@@ -310,7 +311,6 @@ def tile_moe_shr_mlp_gelu_kernel(
         quantize_h("s0")
         activate(r[1])
         activate(s_[1])
-        layer1_whole(r[2], 6)
         y, ys = bank(2, "y0"), bank(0, "ys0")
         layer2(r[0], (0, 1, 2), y)
         layer2(s_[0], (0, 1), ys)
@@ -318,14 +318,13 @@ def tile_moe_shr_mlp_gelu_kernel(
         times_gate(0, y, slice(0, 3), blocks_of(gated[0][:], slice(0, 3)))
         act(ys_rows[0][:], ys[:, : 2 * C])
         nc.vector.tensor_tensor(total[0][:, :C], y[:, N:], gated[0][:, 2 * C :], ADD)
-        activate(r[2])
         turn("b1", 5, act)
         layer1_whole(s_[2], 3)
+        layer1_whole(r[2], 6)
         scatter_sum(0, 0, gated[0][:, :C])
         quantize_h("b1")
         activate(s_[2])
-        layer1_whole(r[3], 2)
-        activate(r[3])
+        activate(r[2])
         y, ys = bank(7, "y1"), bank(1, "ys1")
         layer2(r[1], (0, 1, 2), y)
         layer2(s_[1], (0, 1, 2), ys)
@@ -335,13 +334,15 @@ def tile_moe_shr_mlp_gelu_kernel(
         scatter_scalar(0, 2, total[0])
         times_gate(1, y, slice(0, 3), blocks_of(gated[1][:], slice(0, 3)))
         turn("b2", 4, act)
+        layer1_whole(r[3], 6)
+        activate(r[3])
         layer1_whole(s_[3], 3)
         activate(s_[3])
         quantize_h("b2")
         total[1] = reuse.tile([P, 2 * C], F32, name="total1", offset=rows_at["b2"], align_bytes=64)
         nc.vector.tensor_tensor(total[1][:], ys[:, : 2 * C], gated[1][:, : 2 * C], ADD)
         ys1 = ys
-        y, ys = bank(5, "y2"), bank(6, "ys2")
+        y, ys = bank(5, "y2"), bank(2, "ys2")
         layer2(r[2], (0, 1, 2), y)
         layer2(s_[2], (0, 1, 2), ys)
         scatter_vector(1, 0, total[1][:, :C])
@@ -354,7 +355,7 @@ def tile_moe_shr_mlp_gelu_kernel(
         scatter_scalar(1, 2, last1)
         total[2] = reuse.tile([P, N], F32, name="total2", offset=rows_at["b3"], align_bytes=64)
         nc.vector.tensor_tensor(total[2][:], ys[:, :N], gated[2][:], ADD)
-        y, ys, ys_first = bank(2, "y3"), bank(7, "ys3"), bank(0, "ys3a")
+        y, ys, ys_first = bank(6, "y3"), bank(7, "ys3"), bank(0, "ys3a")
         layer2(r[3], (0, 1, 2), y)
         layer2(s_[3], (1, 2), ys)
         layer2(s_[3], (0,), ys_first)

@@ -257,12 +257,14 @@ def tile_moe_shr_mlp_gelu_kernel(
         load_own(2)
         nc.sync.dma_start(w2_early[:].bitcast(I32), w2_src[:, 2:5])
         nc.sync.dma_start(gate_t[0][:], gate[0:P, 2 * C :])
+        for chunk in range(1, 4):
+            cast(chunk, raw[chunk][:], 0, T, act)
+        late_tiles["sc1"] = reuse.tile([P, 2 * PASSES, H], U8, name="sc1_late", offset=0, align_bytes=64)
+        load_scales(late_tiles["sc1"], w1_sc[:, :, : 2 * PASSES], nc.sync)
         load_own(0)
         load_own(1)
         nc.sync.dma_start(gate_t[1][:], gate[0:P, : 2 * C])
         nc.sync.dma_start(w2_late[:].bitcast(I32), w2_src[:, 0:2])
-        for chunk in range(1, 4):
-            cast(chunk, raw[chunk][:], 0, T, act)
         gather(0, 2 * C, T, planes[:, 2 * C : T])
         gather(0, 0, 2 * C, planes[:, :2 * C])
         for chunk in range(1, 4):
@@ -271,8 +273,6 @@ def tile_moe_shr_mlp_gelu_kernel(
         lay_out(laid0[:], planes[:], 1, 3, act)
         quantize_x(0, 0, 2 * C, laid0[:])
         cast(4, raw[4][:], 0, T, act)
-        late_tiles["sc1"] = reuse.tile([P, 2 * PASSES, H], U8, name="sc1_late", offset=57344, align_bytes=64)
-        load_scales(late_tiles["sc1"], w1_sc[:, :, : 2 * PASSES], nc.gpsimd)
         laid1 = reuse.tile([P, T], U32, name="laid1", offset=57344 + 3072, align_bytes=64)
         lay_out(laid1[:], planes[:], 5, 7, act)
         gather_laid_out(4, 2 * C, T, late[:])
@@ -311,6 +311,7 @@ def tile_moe_shr_mlp_gelu_kernel(
         quantize_h("s0")
         activate(r[1])
         activate(s_[1])
+        layer1_whole(s_[2], 3)
         y, ys = bank(2, "y0"), bank(0, "ys0")
         layer2(r[0], (0, 1, 2), y)
         layer2(s_[0], (0, 1), ys)
@@ -318,12 +319,12 @@ def tile_moe_shr_mlp_gelu_kernel(
         times_gate(0, y, slice(0, 3), blocks_of(gated[0][:], slice(0, 3)))
         act(ys_rows[0][:], ys[:, : 2 * C])
         nc.vector.tensor_tensor(total[0][:, :C], y[:, N:], gated[0][:, 2 * C :], ADD)
+        activate(s_[2])
         turn("b1", 5, act)
-        layer1_whole(s_[2], 3)
         layer1_whole(r[2], 6)
+        h_codes["b1"] = reuse.tile([P, 2 * C], U32, name="codes_b1", offset=own_at[ORDER[2]], align_bytes=64)[:]
         scatter_sum(0, 0, gated[0][:, :C])
         quantize_h("b1")
-        activate(s_[2])
         activate(r[2])
         y, ys = bank(7, "y1"), bank(1, "ys1")
         layer2(r[1], (0, 1, 2), y)
@@ -336,7 +337,7 @@ def tile_moe_shr_mlp_gelu_kernel(
         turn("b2", 4, act)
         layer1_whole(r[3], 6)
         activate(r[3])
-        layer1_whole(s_[3], 3)
+        layer1_whole(s_[3], 7)
         activate(s_[3])
         quantize_h("b2")
         total[1] = reuse.tile([P, 2 * C], F32, name="total1", offset=rows_at["b2"], align_bytes=64)
@@ -355,7 +356,7 @@ def tile_moe_shr_mlp_gelu_kernel(
         scatter_scalar(1, 2, last1)
         total[2] = reuse.tile([P, N], F32, name="total2", offset=rows_at["b3"], align_bytes=64)
         nc.vector.tensor_tensor(total[2][:], ys[:, :N], gated[2][:], ADD)
-        y, ys, ys_first = bank(6, "y3"), bank(7, "ys3"), bank(0, "ys3a")
+        y, ys, ys_first = bank(6, "y3"), bank(3, "ys3"), bank(0, "ys3a")
         layer2(r[3], (0, 1, 2), y)
         layer2(s_[3], (1, 2), ys)
         layer2(s_[3], (0,), ys_first)

from contextlib import ExitStack

import concourse.mybir as mybir
from concourse.masks import make_identity

FLOPS = 2013265920

K, T, E, C, H, N = 1536, 512, 4, 128, 512, 384
P = 128
SHARED = E
PASSES = K // 512
NB = N // P
ORDER = (3, 2, 0, 1)
CAST_SPLIT = 320
END_SPLIT = 160
WIDE = 704

F32 = mybir.dt.float32
BF16 = mybir.dt.bfloat16
I32 = mybir.dt.int32
U32 = mybir.dt.uint32
U16 = mybir.dt.uint16
U8 = mybir.dt.uint8
FP8X4 = mybir.dt.float8_e4m3fn_x4
FP4X4 = mybir.dt.float4_e2m1fn_x4
ADD = mybir.AluOpType.add
MULT = mybir.AluOpType.mult
COPY = mybir.ActivationFunctionType.Copy
GELU = mybir.ActivationFunctionType.Gelu_apprx_tanh


def tile_moe_shr_mlp_gelu_kernel(
    tc, xT, w1_words, w1_scales, w2_words, w2_scales, gate, offs, out
):
    nc = tc.nc
    with ExitStack() as ctx:
        keep = ctx.enter_context(tc.tile_pool(name="keep", bufs=1))
        reuse = ctx.enter_context(tc.tile_pool(name="reuse", bufs=1))
        psum = ctx.enter_context(tc.psum_pool(name="psum", bufs=1))

        offsets = keep.tile([P, E * C // 16], U16, name="offsets")
        sc1_early = keep.tile([P, 3 * PASSES, H], U8, name="sc1_early", align_bytes=64)
        w1_shared = [keep.tile([P, n, 2 * H], U8, name=f"w1_shared{n}", align_bytes=64) for n in (1, 2)]
        own_at = {0: 25600, 1: 12288, 2: 22528, 3: 28672}
        w1_own = [
            reuse.tile([P, PASSES, 2 * H], U8, name=f"w1_own{e}", offset=own_at[e], align_bytes=64) for e in range(E)
        ]
        w2_early = keep.tile([P, 3, 2 * N], U8, name="w2_early", align_bytes=64)
        w2_late = keep.tile([P, 2, 2 * N], U8, name="w2_late", align_bytes=64)
        gate_t = [keep.tile([P, 2 * C], F32, name=f"gate_t{g}") for g in range(2)]
        ident = keep.tile([P, P], F32, name="ident")
        warm = keep.tile([P, 1], F32, name="warm")
        warm_out = keep.tile([P, 1], F32, name="warm_out")
        raw = {c: keep.tile([P, 2, T], F32, name=f"raw{c}", align_bytes=64) for c in (0,)}
        raw[4] = reuse.tile([P, 2, T], F32, name="raw4", offset=57344, align_bytes=64)
        raw[1] = reuse.tile([P, 2, T], F32, name="raw1", offset=0, align_bytes=64)
        raw[2] = reuse.tile([P, 2, T], F32, name="raw2", offset=40960, align_bytes=64)
        raw[3] = reuse.tile([P, 2, T], F32, name="raw3", offset=4096, align_bytes=64)
        raw_end = [
            reuse.tile([P, 2, T // 2], F32, name="raw_5a", offset=36864 - 2048, align_bytes=64),
            keep.tile([P, 2, T // 2], F32, name="raw_5b", align_bytes=64),
        ]
        pairs = keep.tile([P, 6 * T * 2], BF16, name="pairs", align_bytes=64)
        planes = keep.tile([P, 4 * T], U32, name="planes", align_bytes=64)
        late = keep.tile([P, 4 * C], U32, name="late", align_bytes=64)
        laid2 = keep.tile([P, T], U32, name="laid2", align_bytes=64)
        x_codes = [keep.tile([P, PASSES * 2 * C], U32, name=f"x_codes{g}", align_bytes=64) for g in range(2)]
        x_scales = [keep.tile([P, PASSES * 2 * C], U8, name=f"x_scales{g}", align_bytes=64) for g in range(2)]
        out_t = {0: keep.tile([P, T], F32, name="out_t0")}
        h_act = {}
        act_at = {("s", 1): own_at[ORDER[1]], ("s", 3): 45056}
        units = {"r0": [("r", 0)], "s0": [("s", 0)], "b1": [("r", 1), ("s", 1)],
                 "b2": [("r", 2), ("s", 2)], "b3": [("r", 3), ("s", 3)]}
        rows_at = {"r0": 32768, "s0": 33792, "b1": 51200, "b2": 18432, "b3": 47104}
        h_rows = {}
        h_codes = {n: keep.tile([P, C * len(ms)], U32, name=f"codes{n}", align_bytes=64) for n, ms in units.items()}
        h_codes = {n: tile[:] for n, tile in h_codes.items()}
        h_scales = {n: keep.tile([P, C * len(ms)], U8, name=f"hsc{n}", align_bytes=64) for n, ms in units.items()}
        gated = [keep.tile([P, N], F32, name=f"gated{u}") for u in range(E)]
        total = [keep.tile([P, 2 * C], F32, name=f"total{u}") for u in range(E)]
        ys_rows = [keep.tile([P, 2 * C], F32, name=f"ys_rows{u}") for u in range(E)]

        make_identity(nc, ident[:])
        nc.vector.memset(warm[:], 0.0)
        nc.scalar.activation(warm_out[:], warm[:], GELU)
        nc.vector.memset(sc1_early[:].rearrange("p s i -> p (s i)").bitcast(I32), 0)

        x_rows = xT.rearrange("(s p z member) t -> s z p member t", s=PASSES, p=P, z=2)
        w1_src = w1_words.bitcast(I32)
        w2_src = w2_words.bitcast(I32).rearrange("e s p w -> p (e s) w")
        w1_sc = w1_scales.bitcast(I32).rearrange("e s (quad r) w -> r quad (e s) w", r=4)
        w2_sc = w2_scales.bitcast(I32).rearrange("e s (quad r) w -> r quad (e s) w", r=4)

        def load_x(chunk):
            nc.sync.dma_start(raw[chunk][:], x_rows[chunk // 2, chunk % 2])

        def load_scales(dst, src, queue):
            for r in range(4):
                queue.dma_start(dst[r:P:32].bitcast(I32), src[r])

        def load_shared(part, lo, hi):
            nc.sync.dma_start(w1_shared[part][:].bitcast(I32), w1_src[SHARED, lo:hi].rearrange("s p w -> p s w"))

        def load_own(e):
            nc.sync.dma_start(w1_own[e][:].bitcast(I32), w1_src[e].rearrange("s p w -> p s w"))

        late_tiles = {}

        def w1_of(e, s):
            words = w1_shared[min(s, 1)][:, max(s - 1, 0), :] if e == SHARED else w1_own[e][:, s, :]
            if e < 2:
                return words, late_tiles["sc1"][:, e * PASSES + s, :]
            return words, sc1_early[:, (e - 2) * PASSES + s, :]

        def w2_of(e):
            return w2_late[:, e, :] if e < 2 else w2_early[:, e - 2, :]

        def first_pair(chunk):
            return (2 * PASSES - 1 - chunk) * T

        def pairs_of(chunk, lo, hi):
            return pairs[:, 2 * (first_pair(chunk) + lo) : 2 * (first_pair(chunk) + hi)]

        def cast(chunk, src, lo, hi, copy):
            dst = pairs_of(chunk, lo, hi)
            copy(dst.rearrange("p (t member) -> p t member", member=2), src.rearrange("p member t -> p t member"))

        def gather(chunk, lo, hi, dst):
            columns = T if hi - lo < T else WIDE
            window = pairs_of(chunk, 0, columns).bitcast(U32)
            nc.vector.tensor_copy(dst, window.indirect(offsets[:, lo // 16 : hi // 16]))

        def gather_laid_out(chunk, lo, hi, dst):
            gather(chunk, lo, hi, dst.rearrange("p (slot z) -> p slot z", z=2)[:, :, chunk % 2])

        def lay_out(dst, src, first, second, copy):
            halves = src.bitcast(F32).rearrange("p (n slot) -> p slot n", slot=2 * C)
            both = halves[:, :, first : second + 1 : second - first]
            copy(dst.bitcast(F32).rearrange("p (slot z) -> p slot z", z=2), both)

        def quantize_x(g, lo, hi, src):
            nc.vector.quantize_mx(
                out=x_codes[g][:, lo:hi].bitcast(FP8X4), scales=x_scales[g][:, lo:hi], in_=src.bitcast(BF16)
            )

        def bank(n, name):
            return psum.tile([P, 4 * C], F32, name=name, tag=f"bank{n}")

        acc = {}

        def layer1(m, s, n=None):
            kind, u = m
            if s == 0:
                acc[m] = bank(n, f"acc{kind}{u}")
            w, w_scale = w1_of(ORDER[u] if kind == "r" else SHARED, s)
            lo = (2 * s + ORDER[u] % 2) * C
            cols = slice(lo, lo + C)
            nc.tensor.matmul_mx(
                out=acc[m][:],
                lhsT=x_codes[u // 2][:, cols].bitcast(FP8X4),
                lhsT_scale=x_scales[u // 2][:, cols],
                rhs=w.bitcast(FP4X4),
                rhs_scale=w_scale,
                start=(s == 0),
                stop=(s == PASSES - 1),
            )

        def layer1_whole(m, n):
            for s in range(PASSES):
                layer1(m, s, n)

        def activate(m):
            kind, u = m
            if m in act_at:
                h_act[m] = reuse.tile([P, H], BF16, name=f"h_act{kind}{u}", offset=act_at[m], align_bytes=64)
            else:
                h_act[m] = keep.tile([P, H], BF16, name=f"h_act{kind}{u}", align_bytes=64)
            src = acc[m][:].rearrange("p (m v member) -> p v m member", v=2, member=2)
            dst = h_act[m][:].rearrange("p (v m member) -> p v m member", v=2, member=2)
            nc.scalar.activation(dst, src, GELU)

        def turn(unit, n, copy):
            ms = units[unit]
            turned = bank(n, f"turned{unit}")
            for place, m in enumerate(ms):
                h_words = h_act[m][:].bitcast(F32)
                for v in range(2):
                    cols = slice((2 * place + v) * C, (2 * place + v + 1) * C)
                    nc.tensor.transpose(turned[:, cols], h_words[:, v * P : (v + 1) * P], ident[:])
            h_rows[unit] = reuse.tile([P, 2 * C * len(ms)], U32, name=f"rows{unit}", offset=rows_at[unit], align_bytes=64)
            src = turned[:, : 2 * C * len(ms)].rearrange("p (mat v slot) -> p mat slot v", v=2, slot=C)
            dst = h_rows[unit][:].bitcast(F32).rearrange("p (mat slot v) -> p mat slot v", slot=C, v=2)
            copy(dst, src)

        def quantize_h(unit):
            nc.vector.quantize_mx(
                out=h_codes[unit].bitcast(FP8X4), scales=h_scales[unit][:], in_=h_rows[unit][:].bitcast(BF16)
            )

        def layer2(m, blocks, dst):
            kind, u = m
            e = ORDER[u] if kind == "r" else SHARED
            unit, place = (f"{kind}{u}", 0) if u < 1 else (f"b{u}", ("r", "s").index(kind))
            cols = slice(place * C, (place + 1) * C)
            for at, b in enumerate(blocks):
                nc.tensor.matmul_mx(
                    out=dst[:, at * C : (at + 1) * C],
                    lhsT=w2_of(e)[:, 2 * P * b : 2 * P * (b + 1)].bitcast(FP4X4),
                    lhsT_scale=late_tiles["sc2"][:, e, P * b : P * (b + 1)],
                    rhs=h_codes[unit][:, cols].bitcast(FP8X4),
                    rhs_scale=h_scales[unit][:, cols],
                    start=True,
                    stop=True,
                )

        def blocks_of(ap, blocks):
            return ap.rearrange("p (b slot) -> p b slot", slot=C)[:, blocks, :]

        def times_gate(u, y, blocks, dst):
            place = ORDER[u] % 2
            src = blocks_of(y[:, :N], blocks)
            gate_u = gate_t[u // 2][:, place * C : (place + 1) * C].unsqueeze(1).to_broadcast(list(src.shape))
            nc.vector.tensor_tensor(dst, src, gate_u, MULT)

        def where(u, lo=0, hi=C):
            return offsets[:, (ORDER[u] * C + lo) // 16 : (ORDER[u] * C + hi) // 16]

        def scatter_sum(u, b, gated_block):
            nc.vector.tensor_tensor(out_t[b][:].indirect(where(u)), gated_block, ys_rows[u][:, b * C : (b + 1) * C], ADD)

        def scatter_vector(u, b, src, lo=0, hi=C):
            nc.vector.tensor_copy(out_t[b][:].indirect(where(u, lo, hi)), src[:, lo:hi])

        def scatter_scalar(u, b, src, lo=0, hi=C):
            nc.scalar.activation(out_t[b][:].indirect(where(u, lo, hi)), src[:, lo:hi], COPY)

        def store(b):
            nc.sync.dma_start(out[b * P : (b + 1) * P, :], out_t[b][:])

        vec, act = nc.vector.tensor_copy, nc.scalar.copy

        load_x(0)
        nc.sync.dma_start(offsets[:], offs)
        for chunk in range(1, 4):
            load_x(chunk)
        cast(0, raw[0][:, :, :CAST_SPLIT], 0, CAST_SPLIT, vec)
        cast(0, raw[0][:, :, CAST_SPLIT:], CAST_SPLIT, T, act)
        late_tiles["sc2"] = keep.tile([P, E + 1, N], U8, name="sc2", tag="raw0", align_bytes=64)
        load_scales(late_tiles["sc2"], w2_sc, nc.sync)
        load_x(4)
        load_scales(sc1_early, w1_sc[:, :, 2 * PASSES :], nc.sync)
        load_shared(0, 0, 1)
        for half in range(2):
            nc.sync.dma_start(raw_end[half][:], x_rows[2, 1][:, :, half * T // 2 : (half + 1) * T // 2])
        load_own(3)
        load_shared(1, 1, 3)
        load_own(2)
        nc.sync.dma_start(w2_early[:].bitcast(I32), w2_src[:, 2:5])
        nc.sync.dma_start(gate_t[0][:], gate[0:P, 2 * C :])
        for chunk in range(1, 4):
            cast(chunk, raw[chunk][:], 0, T, act)
        late_tiles["sc1"] = reuse.tile([P, 2 * PASSES, H], U8, name="sc1_late", offset=0, align_bytes=64)
        load_scales(late_tiles["sc1"], w1_sc[:, :, : 2 * PASSES], nc.sync)
        load_own(0)
        load_own(1)
        nc.sync.dma_start(gate_t[1][:], gate[0:P, : 2 * C])
        nc.sync.dma_start(w2_late[:].bitcast(I32), w2_src[:, 0:2])
        gather(0, 2 * C, T, planes[:, 2 * C : T])
        gather(0, 0, 2 * C, planes[:, :2 * C])
        for chunk in range(1, 4):
            gather(chunk, 0, T, planes[:, chunk * T : (chunk + 1) * T])
        laid0 = reuse.tile([P, T], U32, name="laid0", offset=6144, align_bytes=64)
        lay_out(laid0[:], planes[:], 1, 3, act)
        quantize_x(0, 0, 2 * C, laid0[:])
        cast(4, raw[4][:], 0, T, act)
        laid1 = reuse.tile([P, T], U32, name="laid1", offset=57344 + 3072, align_bytes=64)
        lay_out(laid1[:], planes[:], 5, 7, act)
        gather_laid_out(4, 2 * C, T, late[:])
        for u in range(2):
            layer1(("s", u), 0, u)
        quantize_x(0, 2 * C, 4 * C, laid1[:])

        cast(5, raw_end[0][:], 0, T // 2, act)
        cast(5, raw_end[1][:], T // 2, T, vec)
        laid_late = reuse.tile([P, 2 * T], U32, name="laid_late", offset=36864 - 128, align_bytes=64)
        late_src = planes[:].bitcast(F32).rearrange("p (s z slot) -> p s slot z", s=2, z=2)[:, :, : 2 * C, :]
        act(laid_late[:].bitcast(F32).rearrange("p (s slot z) -> p s slot z", s=2, z=2), late_src)
        gather_laid_out(5, 3 * C, T, late[:, 2 * C :])
        gather_laid_out(5, 2 * C, 3 * C, late[:, : 2 * C])
        quantize_x(0, 5 * C, 6 * C, late[:, 2 * C :])
        quantize_x(0, 4 * C, 5 * C, late[:, : 2 * C])
        gather(5, 0, 2 * C, late[:, 2 * C :])
        gather(4, 0, 2 * C, late[:, : 2 * C])
        quantize_x(1, 0, 4 * C, laid_late[:])
        lay_out(laid2[:], late[:], 0, 1, vec)
        quantize_x(1, 4 * C, 6 * C, laid2[:])

        r = [("r", u) for u in range(E)]
        s_ = [("s", u) for u in range(E)]
        layer1_whole(r[0], 2)
        activate(r[0])
        for s in (1, 2):
            layer1(s_[0], s)
        activate(s_[0])
        turn("r0", 3, act)
        turn("s0", 4, act)
        layer1_whole(r[1], 5)
        for s in (1, 2):
            layer1(s_[1], s)
        quantize_h("r0")
        quantize_h("s0")
        activate(r[1])
        activate(s_[1])
        layer1_whole(s_[2], 3)
        y, ys = bank(2, "y0"), bank(0, "ys0")
        layer2(r[0], (0, 1, 2), y)
        layer2(s_[0], (0, 1), ys)
        layer2(s_[0], (2,), y[:, N:])
        times_gate(0, y, slice(0, 3), blocks_of(gated[0][:], slice(0, 3)))
        act(ys_rows[0][:], ys[:, : 2 * C])
        nc.vector.tensor_tensor(total[0][:, :C], y[:, N:], gated[0][:, 2 * C :], ADD)
        activate(s_[2])
        turn("b1", 5, act)
        layer1_whole(r[2], 6)
        h_codes["b1"] = reuse.tile([P, 2 * C], U32, name="codes_b1", offset=own_at[ORDER[2]], align_bytes=64)[:]
        scatter_sum(0, 0, gated[0][:, :C])
        quantize_h("b1")
        activate(r[2])
        y, ys = bank(7, "y1"), bank(1, "ys1")
        layer2(r[1], (0, 1, 2), y)
        layer2(s_[1], (0, 1, 2), ys)
        out_t[1] = reuse.tile([P, T], F32, name="out_t1", offset=rows_at["b1"] - 1024, align_bytes=64)
        scatter_sum(0, 1, gated[0][:, C : 2 * C])
        out_t[2] = reuse.tile([P, T], F32, name="out_t2", offset=rows_at["b1"] + 1024, align_bytes=64)
        scatter_scalar(0, 2, total[0])
        times_gate(1, y, slice(0, 3), blocks_of(gated[1][:], slice(0, 3)))
        turn("b2", 4, act)
        layer1_whole(r[3], 6)
        activate(r[3])
        layer1_whole(s_[3], 7)
        activate(s_[3])
        quantize_h("b2")
        total[1] = reuse.tile([P, 2 * C], F32, name="total1", offset=rows_at["b2"], align_bytes=64)
        nc.vector.tensor_tensor(total[1][:], ys[:, : 2 * C], gated[1][:, : 2 * C], ADD)
        ys1 = ys
        y, ys = bank(5, "y2"), bank(2, "ys2")
        layer2(r[2], (0, 1, 2), y)
        layer2(s_[2], (0, 1, 2), ys)
        scatter_vector(1, 0, total[1][:, :C])
        turn("b3", 4, act)
        scatter_scalar(1, 1, total[1][:, C : 2 * C])
        times_gate(2, y, slice(0, 3), blocks_of(gated[2][:], slice(0, 3)))
        last1 = reuse.tile([P, C], F32, name="last1", offset=act_at["s", 3], align_bytes=64)
        nc.vector.tensor_tensor(last1[:], ys1[:, 2 * C : N], gated[1][:, 2 * C :], ADD)
        quantize_h("b3")
        scatter_scalar(1, 2, last1)
        total[2] = reuse.tile([P, N], F32, name="total2", offset=rows_at["b3"], align_bytes=64)
        nc.vector.tensor_tensor(total[2][:], ys[:, :N], gated[2][:], ADD)
        y, ys, ys_first = bank(6, "y3"), bank(3, "ys3"), bank(0, "ys3a")
        layer2(r[3], (0, 1, 2), y)
        layer2(s_[3], (1, 2), ys)
        layer2(s_[3], (0,), ys_first)
        scatter_scalar(2, 1, total[2][:, C : 2 * C])
        scatter_vector(2, 0, total[2][:, :C])
        times_gate(3, y, slice(0, 3), blocks_of(gated[3][:], slice(0, 3)))
        act(ys_rows[3][:, :C], ys_first[:, :C])
        scatter_scalar(2, 2, total[2][:, 2 * C :])
        nc.vector.tensor_tensor(total[3][:], ys[:, : 2 * C], gated[3][:, C:], ADD)
        scatter_sum(3, 0, gated[3][:, :C])
        store(0)
        scatter_scalar(3, 1, total[3], 0, C // 2)
        scatter_scalar(3, 2, total[3][:, C:])
        store(2)
        nc.vector.tensor_copy(out_t[1][:].indirect(where(3, C // 2, C)), total[3][:, C // 2 : C])
        store(1)
